import numpy as np
import ml_dtypes


def mxq(x, axis, fmt="e4m3"):
    dtype, down = {"e4m3": (ml_dtypes.float8_e4m3fn, 7), "e5m2": (ml_dtypes.float8_e5m2, 14)}[fmt]
    v = np.moveaxis(np.asarray(x, np.float32).astype(ml_dtypes.bfloat16).astype(np.float64), axis, -1)
    blocks = v.reshape(v.shape[:-1] + (-1, 32))
    amax = np.abs(blocks).max(-1, keepdims=True)
    byte = np.maximum(np.where(amax > 0, np.frexp(amax)[1] - 1 + 127, 0) - down, 1)
    scale = np.exp2(byte - 127.0)
    codes = (blocks / scale).astype(np.float32).astype(dtype).astype(np.float64)
    return np.moveaxis((codes * scale).reshape(v.shape), -1, axis)


WIDE = False


def mx_kscale(k):
    if not WIDE:
        return np.ones(k)
    levels = np.array([10, -10, 5, -5, 0])
    if k % 512:
        return np.exp2(np.random.permutation(np.resize(levels, k // 32))).repeat(32)
    a = np.empty((k // 512, 16))
    for p in range(k // 512):
        a[p, :8] = np.random.permutation(np.resize(levels, 8))
        for g in range(8):
            far = levels[np.abs(levels - a[p, g]) >= 10]
            a[p, g + 8] = far[np.random.randint(len(far))]
    return np.exp2(a.ravel()).repeat(32)


def f64(x):
    return np.asarray(x).astype(np.float64)


def striped8(idx):
    return np.concatenate([x.reshape(-1, 16).T for x in idx]).astype(np.uint16)


def runs(offs, k):
    lists = np.stack([offs[16 * r : 16 * r + 16].T.reshape(-1) for r in range(8)]).astype(np.int64)
    return lists[np.arange(k) % 512 // 64]


def pack_weight(w):
    k, n = w.shape
    w = f64(np.asarray(w, np.float32).astype(ml_dtypes.bfloat16)).reshape(k // 32, 32, n)
    amax = np.abs(w).max(1)
    byte = np.clip(np.where(amax > 0, np.frexp(amax)[1] - 1 + 127 - 7, 1), 1, 254)
    scaled = (w * np.exp2(127.0 - byte)[:, None, :]).reshape(k, n).astype(np.float32)
    words = np.ascontiguousarray(scaled.reshape(k // 512, 128, 4, n).transpose(0, 1, 3, 2)).astype(ml_dtypes.float8_e4m3fn).view(np.uint8)
    return words, np.ascontiguousarray(byte.astype(np.uint8).reshape(k // 512, 16, n))


def unpack_weight(words, scales):
    g, p, n, _ = words.shape
    vals = np.ascontiguousarray(words).view(ml_dtypes.float8_e4m3fn).astype(np.float64) * np.repeat(np.exp2(scales.astype(np.float64) - 127.0), 8, axis=1)[..., None]
    return vals.transpose(0, 1, 3, 2).reshape(g * 512, n)


K, T, S, V, N, H = 512, 2048, 512, 256, 512, 512


def setup_inputs():
    n = np.random.standard_normal
    s = mx_kscale(K)[:, None]
    u = mx_kscale(S)
    packed_xT = pack_weight(n((K, T)) * s)
    return {
        "x_words": packed_xT[0],
        "x_scales": packed_xT[1],
        "wa": (n((K, H)) / np.sqrt(K) / s).astype(np.float32),
        "wb": (n((K, N)) / np.sqrt(K) / s).astype(np.float32),
        "gt": (np.random.uniform(0.5, 1.5, (S, 1)) * u[:, None]).astype(np.float32),
        "gi": (np.random.uniform(0.5, 1.5, (S, 1)) / u[:, None]).astype(np.float32),
        "offs": striped8(np.stack([np.random.permutation(T)[:S] for _ in range(8)])),
        "cols": striped8(np.stack([np.random.permutation(N)[:V] for _ in range(8)])),
    }


def reference(x_words, x_scales, wa, wb, gt, gi, offs, cols):
    xq = unpack_weight(x_words, x_scales)[np.arange(K)[:, None], runs(offs, K)]
    a = xq.T @ mxq(f64(wa), 0, "e4m3")
    z = f64(gt) * a
    b = xq.T @ mxq(f64(wb), 0, "e4m3")
    z2 = f64(gi) * b
    cv = 0.0625 * ((mxq(z, 0, "e4m3").T @ mxq(z2, 0, "e4m3")))
    return np.tanh(cv[np.arange(H)[:, None], runs(cols, H)])

@@ -1,0 +1,165 @@
+from contextlib import ExitStack
+
+import concourse.mybir as mybir
+
+K, T, S, V, N, H = 512, 2048, 512, 256, 512, 512
+FLOPS = 2 * K * S * H + 2 * K * S * N + 2 * S * H * N
+
+F32 = mybir.dt.float32
+BF16 = mybir.dt.bfloat16
+I32 = mybir.dt.int32
+U32 = mybir.dt.uint32
+U16 = mybir.dt.uint16
+U8 = mybir.dt.uint8
+FP8X4 = mybir.dt.float8_e4m3fn_x4
+ACT = mybir.ActivationFunctionType
+MULT = mybir.AluOpType.mult
+
+P = 128
+PACK = 4
+CH = 128
+HALF = 256
+
+
+def tile_picked_selmom_none_p_kernel(tc, x_words, x_scales, wa, wb, gt, gi, offs, cols, out):
+    nc = tc.nc
+    with ExitStack() as ctx:
+        held = ctx.enter_context(tc.tile_pool(name="held", bufs=1))
+        psum = ctx.enter_context(tc.psum_pool(name="psum", bufs=1))
+
+        def sb(name, shape, dtype):
+            return held.tile(shape, dtype, name=name, align_bytes=64)
+
+        offs_t = sb("offs_t", [P, S // 16], U16)
+        cols_t = sb("cols_t", [P, V // 16], U16)
+        xw = sb("xw", [P, T], U32)
+        xs = sb("xs", [P, T], U8)
+        wa_raw = sb("wa_raw", [P, PACK, H], F32)
+        wb_raw = [sb("wb_raw%d" % h, [P, PACK, HALF], F32) for h in range(2)]
+        gate_a = sb("gate_a", [P, PACK], F32)
+        gate_b = sb("gate_b", [P, PACK], F32)
+        warm = sb("warm", [P, 8], F32)
+
+        nc.scalar.dma_start(out=gate_b[:], in_=gi.rearrange("(p t) o -> p (t o)", t=PACK))
+        nc.scalar.dma_start(out=gate_a[:], in_=gt.rearrange("(p t) o -> p (t o)", t=PACK))
+        nc.vector.memset(warm[:, 0:1], 0.0)
+        nc.scalar.activation(warm[:, 1:2], warm[:, 0:1], ACT.Tanh)
+
+        wb_rows = wb.rearrange("(p j) n -> p j n", j=PACK)
+        nc.sync.dma_start(offs_t[:], offs)
+        scale_rows = x_scales[0].bitcast(I32)
+        nc.sync.dma_start(out=xs[:].bitcast(I32), in_=scale_rows.unsqueeze(1).to_broadcast([16, 8, T // 4]))
+        nc.sync.dma_start(out=xw[:].bitcast(I32), in_=x_words[0].rearrange("p n t -> p (n t)").bitcast(I32))
+        nc.sync.dma_start(out=wb_raw[0][:], in_=wb_rows[:, :, 0:HALF])
+        nc.sync.dma_start(out=wa_raw[:], in_=wa.rearrange("(p j) n -> p j n", j=PACK))
+        nc.sync.dma_start(out=wb_raw[1][:], in_=wb_rows[:, :, HALF:N])
+        nc.sync.dma_start(cols_t[:], cols)
+
+        picked_s = sb("picked_s", [P, S], U8)
+        dealt_s = sb("dealt_s", [P, S], U8)
+        x_plane = sb("x_plane", [P, S], U8)
+        nc.vector.tensor_copy(picked_s[:], xs[:].indirect(offs_t[:]))
+        for dst in (dealt_s, x_plane):
+            nc.vector.tensor_copy(dst[:].rearrange("p (t m) -> p t m", t=PACK), picked_s[:].rearrange("p (m t) -> p t m", t=PACK))
+        for r in range(1, 4):
+            nc.scalar.dma_start(out=x_plane[:].bitcast(I32)[r:P:32, :], in_=dealt_s[:].bitcast(I32)[8 * r : P : 32, :])
+
+        picked_w = sb("picked_w", [P, S], U32)
+        x_codes = sb("x_codes", [P, S], U32)
+        nc.vector.tensor_copy(picked_w[:], xw[:].indirect(offs_t[:]))
+        nc.vector.tensor_copy(
+            x_codes[:].rearrange("p (t c i) -> p c t i", t=PACK, i=4),
+            picked_w[:].rearrange("p (c i t) -> p c t i", t=PACK, i=4),
+        )
+
+        def cast(engine, dst, src):
+            if engine == "S":
+                nc.scalar.copy(dst, src)
+            else:
+                nc.vector.tensor_copy(dst, src)
+
+        def quantize(codes, plane, grouped):
+            nc.vector.quantize_mx(out=codes.bitcast(FP8X4), scales=plane, in_=grouped)
+
+        def project(bank, codes, plane):
+            for t in range(PACK):
+                place = slice(t * CH, (t + 1) * CH)
+                nc.tensor.matmul_mx(
+                    out=bank[:, t, :], lhsT=x_codes[:, place].bitcast(FP8X4), lhsT_scale=x_plane[:, place],
+                    rhs=codes.bitcast(FP8X4), rhs_scale=plane, start=True, stop=True,
+                )
+
+        def weigh(route, name, bank, gate, dst):
+            if route == "V":
+                nc.vector.tensor_tensor(
+                    dst, bank[:].rearrange("p t m -> p m t"), gate[:].unsqueeze(1).to_broadcast([P, CH, PACK]), MULT
+                )
+            else:
+                rows = sb(name + "_rows", [P, PACK, CH], BF16)
+                for t in range(PACK):
+                    nc.scalar.activation(rows[:, t, :], bank[:, t, :], ACT.Copy, scale=gate[:, t : t + 1])
+                nc.vector.tensor_copy(dst.rearrange("p (c i) t -> p c t i", i=4), rows[:].rearrange("p t (c i) -> p c t i", i=4))
+
+        z2_codes = [sb("z2_codes%d" % h, [P, HALF], U32) for h in range(2)]
+        z2_plane = [sb("z2_plane%d" % h, [P, HALF], U8) for h in range(2)]
+
+        def b_weights(h, engines):
+            grouped = sb("wb_grouped%d" % h, [P, HALF, PACK], BF16)
+            codes = sb("wb_codes%d" % h, [P, HALF], U32)
+            plane = sb("wb_plane%d" % h, [P, HALF], U8)
+            for c in range(2):
+                cs = slice(c * CH, (c + 1) * CH)
+                cast(engines[c], grouped[:, cs, :].rearrange("p (c i) j -> p c j i", i=4), wb_raw[h][:, :, cs].rearrange("p j (c i) -> p c j i", i=4))
+            quantize(codes[:], plane[:], grouped[:].rearrange("p n j -> p (n j)"))
+            banks = []
+            for c in range(2):
+                cs = slice(c * CH, (c + 1) * CH)
+                bank = psum.tile([P, PACK, CH], F32, name="b_bank%d" % (2 * h + c))
+                project(bank, codes[:, cs], plane[:, cs])
+                banks.append(bank)
+            return banks
+
+        def b_values(h, banks, routes):
+            grouped = sb("z2_grouped%d" % h, [P, HALF, PACK], BF16)
+            for c in range(2):
+                weigh(routes[c], "z2_%d" % (2 * h + c), banks[c], gate_b, grouped[:, c * CH : (c + 1) * CH, :])
+            quantize(z2_codes[h][:], z2_plane[h][:], grouped[:].rearrange("p n t -> p (n t)"))
+
+        b_values(0, b_weights(0, "SV"), "VS")
+
+        wa_grouped = sb("wa_grouped", [P, PACK, CH, PACK], BF16)
+        wa_codes = sb("wa_codes", [P, H], U32)
+        wa_plane = sb("wa_plane", [P, H], U8)
+        for engine, ms in (("S", slice(0, 64)), ("V", slice(64, 128))):
+            cast(engine, wa_grouped[:].rearrange("p u m j -> p m j u")[:, ms], wa_raw[:].rearrange("p j (m u) -> p m j u", u=PACK)[:, ms])
+        a_banks = []
+        for pair in range(2):
+            ps = slice(pair * HALF, (pair + 1) * HALF)
+            quantize(wa_codes[:, ps], wa_plane[:, ps], wa_grouped[:, 2 * pair : 2 * pair + 2].rearrange("p u m j -> p (u m j)"))
+        b_late = b_weights(1, "VS")
+        for u in range(PACK):
+            us = slice(u * CH, (u + 1) * CH)
+            bank = psum.tile([P, PACK, CH], F32, name="a_bank%d" % u, tag="a_bank%d" % u)
+            project(bank, wa_codes[:, us], wa_plane[:, us])
+            a_banks.append(bank)
+        b_values(1, b_late, "VS")
+
+        out_rows = out.rearrange("(p u) v -> p u v", u=PACK)
+        for u in range(PACK):
+            grouped = sb("z_grouped%d" % u, [P, CH, PACK], BF16)
+            codes = sb("z_codes%d" % u, [P, CH], U32)
+            plane = sb("z_plane%d" % u, [P, CH], U8)
+            weigh("VSSS"[u], "z_%d" % u, a_banks[u], gate_a, grouped[:])
+            quantize(codes[:], plane[:], grouped[:].rearrange("p m t -> p (m t)"))
+            moments = psum.tile([P, N], F32, name="moments%d" % u, tag="a_bank%d" % u)
+            window = sb("window%d" % u, [P, N], F32)
+            for h in range(2):
+                hs = slice(h * HALF, (h + 1) * HALF)
+                nc.tensor.matmul_mx(
+                    out=moments[:, hs], lhsT=codes[:].bitcast(FP8X4), lhsT_scale=plane[:],
+                    rhs=z2_codes[h][:].bitcast(FP8X4), rhs_scale=z2_plane[h][:], start=True, stop=True,
+                )
+            nc.scalar.activation(window[:], moments[:], ACT.Tanh, scale=0.0625)
+            chosen = sb("chosen%d" % u, [P, V], F32)
+            nc.vector.tensor_copy(chosen[:], window[:].indirect(cols_t[:]))
+            nc.sync.dma_start(out=out_rows[:, u, :], in_=chosen[:])

@@ -17,8 +17,12 @@ MULT = mybir.AluOpType.mult
 
 P = 128
 PACK = 4
-CH = 128
-HALF = 256
+CHUNK = 128
+HALF = 2 * CHUNK
+LINE = 4
+LIST_GROUP = 16
+BLOCK_PARTS = 8
+QUADRANT = 32
 
 
 def tile_picked_selmom_none_p_kernel(tc, x_words, x_scales, wa, wb, gt, gi, offs, cols, out):
@@ -27,139 +31,142 @@ def tile_picked_selmom_none_p_kernel(tc, x_words, x_scales, wa, wb, gt, gi, offs
         held = ctx.enter_context(tc.tile_pool(name="held", bufs=1))
         psum = ctx.enter_context(tc.psum_pool(name="psum", bufs=1))
 
-        def sb(name, shape, dtype):
-            return held.tile(shape, dtype, name=name, align_bytes=64)
+        def sbuf(name, shape, dtype, after=None):
+            return held.tile(shape, dtype, name=name, tag=after or name, align_bytes=64)
 
-        offs_t = sb("offs_t", [P, S // 16], U16)
-        cols_t = sb("cols_t", [P, V // 16], U16)
-        xw = sb("xw", [P, T], U32)
-        xs = sb("xs", [P, T], U8)
-        wa_raw = sb("wa_raw", [P, PACK, H], F32)
-        wb_raw = [sb("wb_raw%d" % h, [P, PACK, HALF], F32) for h in range(2)]
-        gate_a = sb("gate_a", [P, PACK], F32)
-        gate_b = sb("gate_b", [P, PACK], F32)
-        warm = sb("warm", [P, 8], F32)
+        def bank(name, shape, after=None):
+            return psum.tile(shape, F32, name=name, tag=after or name)
 
-        nc.scalar.dma_start(out=gate_b[:], in_=gi.rearrange("(p t) o -> p (t o)", t=PACK))
-        nc.scalar.dma_start(out=gate_a[:], in_=gt.rearrange("(p t) o -> p (t o)", t=PACK))
+        def chunk(c, count=1):
+            return slice(c * CHUNK, (c + count) * CHUNK)
+
+        def quantize(codes, plane, grouped):
+            nc.vector.quantize_mx(out=codes.bitcast(FP8X4), scales=plane, in_=grouped.rearrange("p n t -> p (n t)"))
+
+        warm = sbuf("warm", [P, 2], F32)
         nc.vector.memset(warm[:, 0:1], 0.0)
         nc.scalar.activation(warm[:, 1:2], warm[:, 0:1], ACT.Tanh)
 
-        wb_rows = wb.rearrange("(p j) n -> p j n", j=PACK)
-        nc.sync.dma_start(offs_t[:], offs)
+        scale_table = sbuf("scale_table", [P, T], U8)
         scale_rows = x_scales[0].bitcast(I32)
-        nc.sync.dma_start(out=xs[:].bitcast(I32), in_=scale_rows.unsqueeze(1).to_broadcast([16, 8, T // 4]))
-        nc.sync.dma_start(out=xw[:].bitcast(I32), in_=x_words[0].rearrange("p n t -> p (n t)").bitcast(I32))
+        nc.sync.dma_start(out=scale_table[:].bitcast(I32), in_=scale_rows.unsqueeze(1).to_broadcast([P // BLOCK_PARTS, BLOCK_PARTS, T // 4]))
+        offs_list = sbuf("offs_list", [P, S // LIST_GROUP], U16)
+        nc.sync.dma_start(offs_list[:], offs)
+        word_table = sbuf("word_table", [P, T], U32)
+        nc.sync.dma_start(out=word_table[:].bitcast(I32), in_=x_words[0].rearrange("p n t -> p (n t)").bitcast(I32))
+        wa_raw = sbuf("wa_raw", [P, PACK, H], F32)
+        nc.sync.dma_start(out=wa_raw[:], in_=wa.rearrange("(p j) h -> p j h", j=PACK))
+        wb_rows = wb.rearrange("(p j) n -> p j n", j=PACK)
+        wb_raw = [sbuf("wb_raw0", [P, PACK, HALF], F32)]
         nc.sync.dma_start(out=wb_raw[0][:], in_=wb_rows[:, :, 0:HALF])
-        nc.sync.dma_start(out=wa_raw[:], in_=wa.rearrange("(p j) n -> p j n", j=PACK))
-        nc.sync.dma_start(out=wb_raw[1][:], in_=wb_rows[:, :, HALF:N])
-        nc.sync.dma_start(cols_t[:], cols)
+        cols_list = sbuf("cols_list", [P, V // LIST_GROUP], U16)
+        nc.sync.dma_start(cols_list[:], cols)
 
-        picked_s = sb("picked_s", [P, S], U8)
-        dealt_s = sb("dealt_s", [P, S], U8)
-        x_plane = sb("x_plane", [P, S], U8)
-        nc.vector.tensor_copy(picked_s[:], xs[:].indirect(offs_t[:]))
-        for dst in (dealt_s, x_plane):
-            nc.vector.tensor_copy(dst[:].rearrange("p (t m) -> p t m", t=PACK), picked_s[:].rearrange("p (m t) -> p t m", t=PACK))
-        for r in range(1, 4):
-            nc.scalar.dma_start(out=x_plane[:].bitcast(I32)[r:P:32, :], in_=dealt_s[:].bitcast(I32)[8 * r : P : 32, :])
+        picked_scales = sbuf("picked_scales", [P, S], U8)
+        dealt_scales = sbuf("dealt_scales", [P, S], U8)
+        x_plane = sbuf("x_plane", [P, S], U8)
+        nc.vector.tensor_copy(picked_scales[:], scale_table[:].indirect(offs_list[:]))
+        gate_a = sbuf("gate_a", [P, PACK], F32, after="scale_table")
+        nc.sync.dma_start(out=gate_a[:], in_=gt.rearrange("(p t) o -> p (t o)", t=PACK))
+        for dealt in (dealt_scales, x_plane):
+            nc.vector.tensor_copy(dealt[:].rearrange("p (t m) -> p t m", t=PACK), picked_scales[:].rearrange("p (m t) -> p t m", t=PACK))
+        for r in range(1, QUADRANT // BLOCK_PARTS):
+            nc.scalar.dma_start(out=x_plane[:].bitcast(I32)[r:P:QUADRANT, :], in_=dealt_scales[:].bitcast(I32)[BLOCK_PARTS * r : P : QUADRANT, :])
 
-        picked_w = sb("picked_w", [P, S], U32)
-        x_codes = sb("x_codes", [P, S], U32)
-        nc.vector.tensor_copy(picked_w[:], xw[:].indirect(offs_t[:]))
+        picked_words = sbuf("picked_words", [P, S], U32, after="picked_scales")
+        x_codes = sbuf("x_codes", [P, S], U32)
+        nc.vector.tensor_copy(picked_words[:], word_table[:].indirect(offs_list[:]))
         nc.vector.tensor_copy(
-            x_codes[:].rearrange("p (t c i) -> p c t i", t=PACK, i=4),
-            picked_w[:].rearrange("p (c i t) -> p c t i", t=PACK, i=4),
+            x_codes[:].rearrange("p (t c i) -> p c t i", t=PACK, i=LINE),
+            picked_words[:].rearrange("p (c i t) -> p c t i", t=PACK, i=LINE),
         )
+        wb_raw.append(sbuf("wb_raw1", [P, PACK, HALF], F32, after="word_table"))
+        nc.sync.dma_start(out=wb_raw[1][:], in_=wb_rows[:, :, HALF:N])
+        gate_b = sbuf("gate_b", [P, PACK], F32, after="picked_scales")
+        nc.sync.dma_start(out=gate_b[:], in_=gi.rearrange("(p t) o -> p (t o)", t=PACK))
 
-        def cast(engine, dst, src):
-            if engine == "S":
-                nc.scalar.copy(dst, src)
-            else:
-                nc.vector.tensor_copy(dst, src)
-
-        def quantize(codes, plane, grouped):
-            nc.vector.quantize_mx(out=codes.bitcast(FP8X4), scales=plane, in_=grouped)
-
-        def project(bank, codes, plane):
+        def project(product, codes, plane):
             for t in range(PACK):
-                place = slice(t * CH, (t + 1) * CH)
                 nc.tensor.matmul_mx(
-                    out=bank[:, t, :], lhsT=x_codes[:, place].bitcast(FP8X4), lhsT_scale=x_plane[:, place],
+                    out=product[:, t, :], lhsT=x_codes[:, chunk(t)].bitcast(FP8X4), lhsT_scale=x_plane[:, chunk(t)],
                     rhs=codes.bitcast(FP8X4), rhs_scale=plane, start=True, stop=True,
                 )
 
-        def weigh(route, name, bank, gate, dst):
-            if route == "V":
-                nc.vector.tensor_tensor(
-                    dst, bank[:].rearrange("p t m -> p m t"), gate[:].unsqueeze(1).to_broadcast([P, CH, PACK]), MULT
+        def weigh_on_vector(grouped, product, gate):
+            nc.vector.tensor_tensor(grouped, product[:].rearrange("p t n -> p n t"), gate[:].unsqueeze(1).to_broadcast([P, CHUNK, PACK]), MULT)
+
+        def weigh_on_scalar(grouped, product, gate, name):
+            rows = sbuf(name, [P, PACK, CHUNK], BF16)
+            for t in range(PACK):
+                nc.scalar.activation(rows[:, t, :], product[:, t, :], ACT.Copy, scale=gate[:, t : t + 1])
+            nc.vector.tensor_copy(grouped.rearrange("p (c i) t -> p c t i", i=LINE), rows[:].rearrange("p t (c i) -> p c t i", i=LINE))
+
+        wa_grouped = sbuf("wa_grouped", [P, H, PACK], BF16)
+        wa_codes = sbuf("wa_codes", [P, H], U32)
+        wa_plane = sbuf("wa_plane", [P, H], U8)
+        dealt_out = wa_grouped[:].rearrange("p (u m) j -> p m j u", u=PACK)
+        dealt_in = wa_raw[:].rearrange("p j (m u) -> p m j u", u=PACK)
+        nc.vector.tensor_copy(dealt_out[:, :, :, 0:2], dealt_in[:, :, :, 0:2])
+        nc.scalar.copy(dealt_out[:, :, :, 2:4], dealt_in[:, :, :, 2:4])
+        a_product = {}
+        for u in (0, 1):
+            quantize(wa_codes[:, chunk(u)], wa_plane[:, chunk(u)], wa_grouped[:, chunk(u), :])
+            a_product[u] = bank("a_product%d" % u, [P, PACK, CHUNK])
+            project(a_product[u], wa_codes[:, chunk(u)], wa_plane[:, chunk(u)])
+
+        wb_codes = sbuf("wb_codes", [P, N], U32)
+        wb_plane = sbuf("wb_plane", [P, N], U8)
+        b_product = {}
+        for half in range(2):
+            pair = (2 * half, 2 * half + 1)
+            wb_grouped = {c: sbuf("wb_grouped%d" % c, [P, CHUNK, PACK], BF16) for c in pair}
+            for c in pair:
+                nc.scalar.copy(
+                    wb_grouped[c][:].rearrange("p (c i) j -> p c j i", i=LINE),
+                    wb_raw[half][:, :, chunk(c % 2)].rearrange("p j (c i) -> p c j i", i=LINE),
                 )
-            else:
-                rows = sb(name + "_rows", [P, PACK, CH], BF16)
-                for t in range(PACK):
-                    nc.scalar.activation(rows[:, t, :], bank[:, t, :], ACT.Copy, scale=gate[:, t : t + 1])
-                nc.vector.tensor_copy(dst.rearrange("p (c i) t -> p c t i", i=4), rows[:].rearrange("p t (c i) -> p c t i", i=4))
+            for c in pair:
+                quantize(wb_codes[:, chunk(c)], wb_plane[:, chunk(c)], wb_grouped[c][:])
+            for c in pair:
+                b_product[c] = bank("b_product%d" % c, [P, PACK, CHUNK])
+                project(b_product[c], wb_codes[:, chunk(c)], wb_plane[:, chunk(c)])
+        quantize(wa_codes[:, chunk(2, 2)], wa_plane[:, chunk(2, 2)], wa_grouped[:, chunk(2, 2), :])
 
-        z2_codes = [sb("z2_codes%d" % h, [P, HALF], U32) for h in range(2)]
-        z2_plane = [sb("z2_plane%d" % h, [P, HALF], U8) for h in range(2)]
+        z2_codes = sbuf("z2_codes", [P, N], U32)
+        z2_plane = sbuf("z2_plane", [P, N], U8)
+        for half, after in enumerate(("wb_grouped3", None)):
+            z2_grouped = sbuf("z2_grouped%d" % half, [P, HALF, PACK], BF16, after=after)
+            weigh_on_scalar(z2_grouped[:, chunk(0), :], b_product[2 * half], gate_b, "z2_rows%d" % half)
+            weigh_on_vector(z2_grouped[:, chunk(1), :], b_product[2 * half + 1], gate_b)
+            quantize(z2_codes[:, chunk(2 * half, 2)], z2_plane[:, chunk(2 * half, 2)], z2_grouped[:])
 
-        def b_weights(h, engines):
-            grouped = sb("wb_grouped%d" % h, [P, HALF, PACK], BF16)
-            codes = sb("wb_codes%d" % h, [P, HALF], U32)
-            plane = sb("wb_plane%d" % h, [P, HALF], U8)
-            for c in range(2):
-                cs = slice(c * CH, (c + 1) * CH)
-                cast(engines[c], grouped[:, cs, :].rearrange("p (c i) j -> p c j i", i=4), wb_raw[h][:, :, cs].rearrange("p j (c i) -> p c j i", i=4))
-            quantize(codes[:], plane[:], grouped[:].rearrange("p n j -> p (n j)"))
-            banks = []
-            for c in range(2):
-                cs = slice(c * CH, (c + 1) * CH)
-                bank = psum.tile([P, PACK, CH], F32, name="b_bank%d" % (2 * h + c))
-                project(bank, codes[:, cs], plane[:, cs])
-                banks.append(bank)
-            return banks
+        for u in (2, 3):
+            a_product[u] = bank("a_product%d" % u, [P, PACK, CHUNK], after="b_product%d" % (2 * (u - 2)))
+            project(a_product[u], wa_codes[:, chunk(u)], wa_plane[:, chunk(u)])
 
-        def b_values(h, banks, routes):
-            grouped = sb("z2_grouped%d" % h, [P, HALF, PACK], BF16)
-            for c in range(2):
-                weigh(routes[c], "z2_%d" % (2 * h + c), banks[c], gate_b, grouped[:, c * CH : (c + 1) * CH, :])
-            quantize(z2_codes[h][:], z2_plane[h][:], grouped[:].rearrange("p n t -> p (n t)"))
-
-        b_values(0, b_weights(0, "SV"), "VS")
-
-        wa_grouped = sb("wa_grouped", [P, PACK, CH, PACK], BF16)
-        wa_codes = sb("wa_codes", [P, H], U32)
-        wa_plane = sb("wa_plane", [P, H], U8)
-        for engine, ms in (("S", slice(0, 64)), ("V", slice(64, 128))):
-            cast(engine, wa_grouped[:].rearrange("p u m j -> p m j u")[:, ms], wa_raw[:].rearrange("p j (m u) -> p m j u", u=PACK)[:, ms])
-        a_banks = []
-        for pair in range(2):
-            ps = slice(pair * HALF, (pair + 1) * HALF)
-            quantize(wa_codes[:, ps], wa_plane[:, ps], wa_grouped[:, 2 * pair : 2 * pair + 2].rearrange("p u m j -> p (u m j)"))
-        b_late = b_weights(1, "VS")
+        z_codes = sbuf("z_codes", [P, H], U32)
+        z_plane = sbuf("z_plane", [P, H], U8)
         for u in range(PACK):
-            us = slice(u * CH, (u + 1) * CH)
-            bank = psum.tile([P, PACK, CH], F32, name="a_bank%d" % u, tag="a_bank%d" % u)
-            project(bank, wa_codes[:, us], wa_plane[:, us])
-            a_banks.append(bank)
-        b_values(1, b_late, "VS")
+            if u < 2:
+                z_grouped = sbuf("z_grouped%d" % u, [P, CHUNK, PACK], BF16, after="wb_grouped%d" % (2 * u))
+                weigh_on_vector(z_grouped[:], a_product[u], gate_a)
+            else:
+                z_grouped = sbuf("z_grouped%d" % u, [P, CHUNK, PACK], BF16)
+                weigh_on_scalar(z_grouped[:], a_product[u], gate_a, "z_rows%d" % u)
+            quantize(z_codes[:, chunk(u)], z_plane[:, chunk(u)], z_grouped[:])
 
+        halves = [chunk(0, 2), chunk(2, 2)]
         out_rows = out.rearrange("(p u) v -> p u v", u=PACK)
         for u in range(PACK):
-            grouped = sb("z_grouped%d" % u, [P, CH, PACK], BF16)
-            codes = sb("z_codes%d" % u, [P, CH], U32)
-            plane = sb("z_plane%d" % u, [P, CH], U8)
-            weigh("VSSS"[u], "z_%d" % u, a_banks[u], gate_a, grouped[:])
-            quantize(codes[:], plane[:], grouped[:].rearrange("p m t -> p (m t)"))
-            moments = psum.tile([P, N], F32, name="moments%d" % u, tag="a_bank%d" % u)
-            window = sb("window%d" % u, [P, N], F32)
-            for h in range(2):
-                hs = slice(h * HALF, (h + 1) * HALF)
+            moments = bank("moments%d" % u, [P, N], after="a_product%d" % u if u < 2 else None)
+            window = sbuf("window%d" % u, [P, N], F32)
+            for piece in halves:
                 nc.tensor.matmul_mx(
-                    out=moments[:, hs], lhsT=codes[:].bitcast(FP8X4), lhsT_scale=plane[:],
-                    rhs=z2_codes[h][:].bitcast(FP8X4), rhs_scale=z2_plane[h][:], start=True, stop=True,
+                    out=moments[:, piece], lhsT=z_codes[:, chunk(u)].bitcast(FP8X4), lhsT_scale=z_plane[:, chunk(u)],
+                    rhs=z2_codes[:, piece].bitcast(FP8X4), rhs_scale=z2_plane[:, piece], start=True, stop=True,
                 )
-            nc.scalar.activation(window[:], moments[:], ACT.Tanh, scale=0.0625)
-            chosen = sb("chosen%d" % u, [P, V], F32)
-            nc.vector.tensor_copy(chosen[:], window[:].indirect(cols_t[:]))
+            for piece in halves:
+                nc.scalar.activation(window[:, piece], moments[:, piece], ACT.Tanh, scale=0.0625)
+            chosen = sbuf("chosen%d" % u, [P, V], F32)
+            nc.vector.tensor_copy(chosen[:], window[:].indirect(cols_list[:]))
             nc.sync.dma_start(out=out_rows[:, u, :], in_=chosen[:])

@@ -19,6 +19,7 @@ P = 128
 PACK = 4
 CHUNK = 128
 HALF = 2 * CHUNK
+VECTOR_CHUNK = 1
 LINE = 4
 LIST_GROUP = 16
 BLOCK_PARTS = 8
@@ -121,9 +122,10 @@ def tile_picked_selmom_none_p_kernel(tc, x_words, x_scales, wa, wb, gt, gi, offs
             pair = (2 * half, 2 * half + 1)
             wb_grouped = {c: sbuf("wb_grouped%d" % c, [P, CHUNK, PACK], BF16) for c in pair}
             for c in pair:
-                nc.scalar.copy(
-                    wb_grouped[c][:].rearrange("p (c i) j -> p c j i", i=LINE),
-                    wb_raw[half][:, :, chunk(c % 2)].rearrange("p j (c i) -> p c j i", i=LINE),
+                copy = nc.vector.tensor_copy if c == VECTOR_CHUNK else nc.scalar.copy
+                copy(
+                    wb_grouped[c][:].rearrange("p (g i) j -> p g j i", i=LINE),
+                    wb_raw[half][:, :, chunk(c % 2)].rearrange("p j (g i) -> p g j i", i=LINE),
                 )
             for c in pair:
                 quantize(wb_codes[:, chunk(c)], wb_plane[:, chunk(c)], wb_grouped[c][:])
@@ -148,7 +150,7 @@ def tile_picked_selmom_none_p_kernel(tc, x_words, x_scales, wa, wb, gt, gi, offs
         z_plane = sbuf("z_plane", [P, H], U8)
         for u in range(PACK):
             if u < 2:
-                z_grouped = sbuf("z_grouped%d" % u, [P, CHUNK, PACK], BF16, after="wb_grouped%d" % (2 * u))
+                z_grouped = sbuf("z_grouped%d" % u, [P, CHUNK, PACK], BF16, after="wb_grouped%d" % (u + 1))
                 weigh_on_vector(z_grouped[:], a_product[u], gate_a)
             else:
                 z_grouped = sbuf("z_grouped%d" % u, [P, CHUNK, PACK], BF16)

@@ -19,21 +19,25 @@ P = 128
 PACK = 4
 CHUNK = 128
 HALF = 2 * CHUNK
-VECTOR_CHUNK = 1
 LINE = 4
 LIST_GROUP = 16
 BLOCK_PARTS = 8
 QUADRANT = 32
+ROWS = CHUNK // PACK
 
 
 def tile_picked_selmom_none_p_kernel(tc, x_words, x_scales, wa, wb, gt, gi, offs, cols, out):
     nc = tc.nc
     with ExitStack() as ctx:
         held = ctx.enter_context(tc.tile_pool(name="held", bufs=1))
+        placed = ctx.enter_context(tc.tile_pool(name="placed", bufs=1))
         psum = ctx.enter_context(tc.psum_pool(name="psum", bufs=1))
 
         def sbuf(name, shape, dtype, after=None):
             return held.tile(shape, dtype, name=name, tag=after or name, align_bytes=64)
+
+        def at(name, shape, dtype, offset):
+            return placed.tile(shape, dtype, name=name, tag=name, align_bytes=64, offset=offset)
 
         def bank(name, shape, after=None):
             return psum.tile(shape, F32, name=name, tag=after or name)
@@ -41,8 +45,48 @@ def tile_picked_selmom_none_p_kernel(tc, x_words, x_scales, wa, wb, gt, gi, offs
         def chunk(c, count=1):
             return slice(c * CHUNK, (c + count) * CHUNK)
 
-        def quantize(codes, plane, grouped):
-            nc.vector.quantize_mx(out=codes.bitcast(FP8X4), scales=plane, in_=grouped.rearrange("p n t -> p (n t)"))
+        def quantize(name, columns, grouped):
+            nc.vector.quantize_mx(out=codes[name][:, columns].bitcast(FP8X4), scales=plane[name][:, columns], in_=grouped.rearrange("p n t -> p (n t)"))
+
+        def round_columns(copy, grouped, raw):
+            copy(grouped.rearrange("p (g i) j -> p g j i", i=LINE), raw.rearrange("p j (g i) -> p g j i", i=LINE))
+
+        def project(name, c, after=None):
+            product[name, c] = bank("%s_product%d" % (name, c), [P, PACK, CHUNK], after=after)
+            for t in range(PACK):
+                nc.tensor.matmul_mx(
+                    out=product[name, c][:, t, :], lhsT=x_codes[:, chunk(t)].bitcast(FP8X4), lhsT_scale=x_plane[:, chunk(t)],
+                    rhs=codes[name][:, chunk(c)].bitcast(FP8X4), rhs_scale=plane[name][:, chunk(c)], start=True, stop=True,
+                )
+
+        def weigh(grouped, name, c):
+            nc.vector.tensor_tensor(grouped, product[name, c][:].rearrange("p t n -> p n t"), gate[name][:].unsqueeze(1).to_broadcast([P, CHUNK, PACK]), MULT)
+
+        def weigh_rows(name, c, after=None):
+            rows = sbuf("%s_rows%d" % (name, c), [P, PACK, CHUNK], BF16, after=after)
+            for t in range(PACK):
+                nc.scalar.activation(rows[:, t, :], product[name, c][:, t, :], ACT.Copy, scale=gate[name][:, t : t + 1])
+            return rows
+
+        def interleave(grouped, rows):
+            nc.vector.tensor_copy(grouped.rearrange("p (g i) t -> p g t i", i=LINE), rows[:].rearrange("p t (g i) -> p g t i", i=LINE))
+
+        def moments(tiles, columns, after):
+            width = columns.stop - columns.start
+            sums = bank("moments%d_%d" % (tiles[0], columns.start), [P, len(tiles), width], after=after)
+            for i, u in enumerate(tiles):
+                nc.tensor.matmul_mx(
+                    out=sums[:, i, :], lhsT=codes["z"][:, chunk(u)].bitcast(FP8X4), lhsT_scale=plane["z"][:, chunk(u)],
+                    rhs=codes["z2"][:, columns].bitcast(FP8X4), rhs_scale=plane["z2"][:, columns], start=True, stop=True,
+                )
+            for i, u in enumerate(tiles):
+                nc.scalar.activation(window[u][:, columns], sums[:, i, :], ACT.Tanh, scale=0.0625)
+
+        codes = {name: sbuf(name + "_codes", [P, H], U32) for name in ("wa", "wb", "z", "z2")}
+        plane = {name: sbuf(name + "_plane", [P, H], U8) for name in ("wa", "wb", "z", "z2")}
+        window = [sbuf("window%d" % u, [P, N], F32) for u in range(PACK)]
+        product = {}
+        gate = {}
 
         warm = sbuf("warm", [P, 2], F32)
         nc.vector.memset(warm[:, 0:1], 0.0)
@@ -55,120 +99,98 @@ def tile_picked_selmom_none_p_kernel(tc, x_words, x_scales, wa, wb, gt, gi, offs
         nc.sync.dma_start(offs_list[:], offs)
         word_table = sbuf("word_table", [P, T], U32)
         nc.sync.dma_start(out=word_table[:].bitcast(I32), in_=x_words[0].rearrange("p n t -> p (n t)").bitcast(I32))
-        wa_raw = sbuf("wa_raw", [P, PACK, H], F32)
-        nc.sync.dma_start(out=wa_raw[:], in_=wa.rearrange("(p j) h -> p j h", j=PACK))
+        wa_rows = wa.rearrange("(p j) h -> p j h", j=PACK)
         wb_rows = wb.rearrange("(p j) n -> p j n", j=PACK)
-        wb_raw = [sbuf("wb_raw0", [P, PACK, HALF], F32)]
-        nc.sync.dma_start(out=wb_raw[0][:], in_=wb_rows[:, :, 0:HALF])
+        wb_raw = [sbuf("wb_raw%d" % half, [P, PACK, HALF], F32) for half in range(2)]
+        for half in range(2):
+            nc.sync.dma_start(out=wb_raw[half][:], in_=wb_rows[:, :, chunk(2 * half, 2)])
         cols_list = sbuf("cols_list", [P, V // LIST_GROUP], U16)
         nc.sync.dma_start(cols_list[:], cols)
 
-        picked_scales = sbuf("picked_scales", [P, S], U8)
-        dealt_scales = sbuf("dealt_scales", [P, S], U8)
+        half_bytes = PACK * HALF * 4
+        picked_scales = at("picked_scales", [P, S], U8, half_bytes - 64)
         x_plane = sbuf("x_plane", [P, S], U8)
         nc.vector.tensor_copy(picked_scales[:], scale_table[:].indirect(offs_list[:]))
-        gate_a = sbuf("gate_a", [P, PACK], F32, after="scale_table")
-        nc.sync.dma_start(out=gate_a[:], in_=gt.rearrange("(p t) o -> p (t o)", t=PACK))
-        for dealt in (dealt_scales, x_plane):
-            nc.vector.tensor_copy(dealt[:].rearrange("p (t m) -> p t m", t=PACK), picked_scales[:].rearrange("p (m t) -> p t m", t=PACK))
+        nc.vector.tensor_copy(x_plane[:].rearrange("p (t m) -> p t m", t=PACK), picked_scales[:].rearrange("p (m t) -> p t m", t=PACK))
         for r in range(1, QUADRANT // BLOCK_PARTS):
-            nc.scalar.dma_start(out=x_plane[:].bitcast(I32)[r:P:QUADRANT, :], in_=dealt_scales[:].bitcast(I32)[BLOCK_PARTS * r : P : QUADRANT, :])
+            nc.sync.dma_start(out=x_plane[:].bitcast(I32)[r:P:QUADRANT, :], in_=x_plane[:].bitcast(I32)[BLOCK_PARTS * r : P : QUADRANT, :])
+        wa_raw = [at("wa_raw0", [P, PACK, HALF], F32, 0), at("wa_raw1", [P, PACK, HALF], F32, half_bytes + 384)]
+        for half in range(2):
+            nc.sync.dma_start(out=wa_raw[half][:], in_=wa_rows[:, :, chunk(2 * half, 2)])
+            if half == 0:
+                gate["wb"] = at("gate_b", [P, PACK], F32, half_bytes + 192)
+                nc.sync.dma_start(out=gate["wb"][:], in_=gi.rearrange("(p t) o -> p (t o)", t=PACK))
+        gate["wa"] = at("gate_a", [P, PACK], F32, half_bytes + 128)
+        nc.sync.dma_start(out=gate["wa"][:], in_=gt.rearrange("(p t) o -> p (t o)", t=PACK))
 
-        picked_words = sbuf("picked_words", [P, S], U32, after="picked_scales")
+        picked_words = sbuf("picked_words", [P, S], U32)
         x_codes = sbuf("x_codes", [P, S], U32)
+        wb_grouped = [sbuf("wb_grouped%d" % c, [P, CHUNK, PACK], BF16) for c in range(PACK)]
         nc.vector.tensor_copy(picked_words[:], word_table[:].indirect(offs_list[:]))
+        round_columns(nc.scalar.copy, wb_grouped[0][:], wb_raw[0][:, :, chunk(0)])
+        round_columns(nc.vector.tensor_copy, wb_grouped[1][:], wb_raw[0][:, :, chunk(1)])
         nc.vector.tensor_copy(
             x_codes[:].rearrange("p (t c i) -> p c t i", t=PACK, i=LINE),
             picked_words[:].rearrange("p (c i t) -> p c t i", t=PACK, i=LINE),
         )
-        wb_raw.append(sbuf("wb_raw1", [P, PACK, HALF], F32, after="word_table"))
-        nc.sync.dma_start(out=wb_raw[1][:], in_=wb_rows[:, :, HALF:N])
-        gate_b = sbuf("gate_b", [P, PACK], F32, after="picked_scales")
-        nc.sync.dma_start(out=gate_b[:], in_=gi.rearrange("(p t) o -> p (t o)", t=PACK))
+        for c in range(2):
+            quantize("wb", chunk(c), wb_grouped[c][:])
+            project("wb", c)
+        round_columns(nc.scalar.copy, wb_grouped[2][:], wb_raw[1][:, :, chunk(0)])
+        round_columns(nc.vector.tensor_copy, wb_grouped[3][:], wb_raw[1][:, :, chunk(1)])
+        for c in (3, 2):
+            quantize("wb", chunk(c), wb_grouped[c][:])
+            project("wb", c)
 
-        def project(product, codes, plane):
-            for t in range(PACK):
-                nc.tensor.matmul_mx(
-                    out=product[:, t, :], lhsT=x_codes[:, chunk(t)].bitcast(FP8X4), lhsT_scale=x_plane[:, chunk(t)],
-                    rhs=codes.bitcast(FP8X4), rhs_scale=plane, start=True, stop=True,
-                )
-
-        def weigh_on_vector(grouped, product, gate):
-            nc.vector.tensor_tensor(grouped, product[:].rearrange("p t n -> p n t"), gate[:].unsqueeze(1).to_broadcast([P, CHUNK, PACK]), MULT)
-
-        def weigh_on_scalar(grouped, product, gate, name):
-            rows = sbuf(name, [P, PACK, CHUNK], BF16)
-            for t in range(PACK):
-                nc.scalar.activation(rows[:, t, :], product[:, t, :], ACT.Copy, scale=gate[:, t : t + 1])
-            nc.vector.tensor_copy(grouped.rearrange("p (c i) t -> p c t i", i=LINE), rows[:].rearrange("p t (c i) -> p c t i", i=LINE))
-
-        wa_grouped = sbuf("wa_grouped", [P, H, PACK], BF16)
-        wa_codes = sbuf("wa_codes", [P, H], U32)
-        wa_plane = sbuf("wa_plane", [P, H], U8)
-        dealt_out = wa_grouped[:].rearrange("p (u m) j -> p m j u", u=PACK)
-        dealt_in = wa_raw[:].rearrange("p j (m u) -> p m j u", u=PACK)
-        nc.vector.tensor_copy(dealt_out[:, :, :, 0:2], dealt_in[:, :, :, 0:2])
-        nc.scalar.copy(dealt_out[:, :, :, 2:4], dealt_in[:, :, :, 2:4])
-        a_product = {}
-        for u in (0, 1):
-            quantize(wa_codes[:, chunk(u)], wa_plane[:, chunk(u)], wa_grouped[:, chunk(u), :])
-            a_product[u] = bank("a_product%d" % u, [P, PACK, CHUNK])
-            project(a_product[u], wa_codes[:, chunk(u)], wa_plane[:, chunk(u)])
-
-        wb_codes = sbuf("wb_codes", [P, N], U32)
-        wb_plane = sbuf("wb_plane", [P, N], U8)
-        b_product = {}
+        wa_grouped = [sbuf("wa_grouped%d" % pair, [P, 2, CHUNK, PACK], BF16) for pair in range(2)]
         for half in range(2):
-            pair = (2 * half, 2 * half + 1)
-            wb_grouped = {c: sbuf("wb_grouped%d" % c, [P, CHUNK, PACK], BF16) for c in pair}
-            for c in pair:
-                copy = nc.vector.tensor_copy if c == VECTOR_CHUNK else nc.scalar.copy
-                copy(
-                    wb_grouped[c][:].rearrange("p (g i) j -> p g j i", i=LINE),
-                    wb_raw[half][:, :, chunk(c % 2)].rearrange("p j (g i) -> p g j i", i=LINE),
-                )
-            for c in pair:
-                quantize(wb_codes[:, chunk(c)], wb_plane[:, chunk(c)], wb_grouped[c][:])
-            for c in pair:
-                b_product[c] = bank("b_product%d" % c, [P, PACK, CHUNK])
-                project(b_product[c], wb_codes[:, chunk(c)], wb_plane[:, chunk(c)])
-        quantize(wa_codes[:, chunk(2, 2)], wa_plane[:, chunk(2, 2)], wa_grouped[:, chunk(2, 2), :])
+            for pair in range(2):
+                dealt_out = wa_grouped[pair][:, :, half * 64 : (half + 1) * 64, :].rearrange("p u m j -> p m j u")
+                dealt_in = wa_raw[half][:].rearrange("p j (m u) -> p m j u", u=PACK)
+                nc.scalar.copy(dealt_out, dealt_in[:, :, :, 2 * pair : 2 * pair + 2])
 
-        z2_codes = sbuf("z2_codes", [P, N], U32)
-        z2_plane = sbuf("z2_plane", [P, N], U8)
-        for half, after in enumerate(("wb_grouped3", None)):
-            z2_grouped = sbuf("z2_grouped%d" % half, [P, HALF, PACK], BF16, after=after)
-            weigh_on_scalar(z2_grouped[:, chunk(0), :], b_product[2 * half], gate_b, "z2_rows%d" % half)
-            weigh_on_vector(z2_grouped[:, chunk(1), :], b_product[2 * half + 1], gate_b)
-            quantize(z2_codes[:, chunk(2 * half, 2)], z2_plane[:, chunk(2 * half, 2)], z2_grouped[:])
-
-        for u in (2, 3):
-            a_product[u] = bank("a_product%d" % u, [P, PACK, CHUNK], after="b_product%d" % (2 * (u - 2)))
-            project(a_product[u], wa_codes[:, chunk(u)], wa_plane[:, chunk(u)])
-
-        z_codes = sbuf("z_codes", [P, H], U32)
-        z_plane = sbuf("z_plane", [P, H], U8)
-        for u in range(PACK):
-            if u < 2:
-                z_grouped = sbuf("z_grouped%d" % u, [P, CHUNK, PACK], BF16, after="wb_grouped%d" % (u + 1))
-                weigh_on_vector(z_grouped[:], a_product[u], gate_a)
+        z2_first = sbuf("z2_first", [P, HALF, PACK], BF16)
+        for c in (0, 1):
+            weigh(z2_first[:, chunk(c), :], "wb", c)
+        z2_third = sbuf("z2_third", [P, CHUNK, PACK], BF16)
+        weigh(z2_third[:], "wb", 3)
+        quantize("wa", chunk(0, 2), wa_grouped[0][:].rearrange("p u m j -> p (u m) j"))
+        quantize("z2", chunk(0, 2), z2_first[:])
+        quantize("wa", chunk(2, 2), wa_grouped[1][:].rearrange("p u m j -> p (u m) j"))
+        quantize("z2", chunk(3), z2_third[:])
+        z2_last = sbuf("z2_last", [P, CHUNK, PACK], BF16, after="wa_grouped0")
+        weigh(z2_last[:], "wb", 2)
+        for u in (0, 1, 2, 3):
+            project("wa", u)
+        z_grouped = [sbuf("z_grouped%d" % u, [P, CHUNK, PACK], BF16) for u in range(PACK)]
+        rows = {u: weigh_rows("wa", u) for u in (1, 3)}
+        def finish(u):
+            if u in rows:
+                interleave(z_grouped[u][:], rows[u])
             else:
-                z_grouped = sbuf("z_grouped%d" % u, [P, CHUNK, PACK], BF16)
-                weigh_on_scalar(z_grouped[:], a_product[u], gate_a, "z_rows%d" % u)
-            quantize(z_codes[:, chunk(u)], z_plane[:, chunk(u)], z_grouped[:])
+                weigh(z_grouped[u][:], "wa", u)
+        order = (0, 1, 2, 3)
+        finish(order[0])
+        quantize("z2", chunk(2), z2_last[:])
+        for i, u in enumerate(order):
+            if 0 < i < 3:
+                finish(order[i + 1])
+            quantize("z", chunk(u), z_grouped[u][:])
+            if i == 0:
+                finish(order[1])
+            if i < 3:
+                moments((u,), chunk(0, 4), "wb_product%d" % i)
+            else:
+                moments((u,), chunk(0, 2), "wb_product%d" % i)
+                moments((u,), chunk(2, 2), "wa_product0")
 
-        halves = [chunk(0, 2), chunk(2, 2)]
         out_rows = out.rearrange("(p u) v -> p u v", u=PACK)
-        for u in range(PACK):
-            moments = bank("moments%d" % u, [P, N], after="a_product%d" % u if u < 2 else None)
-            window = sbuf("window%d" % u, [P, N], F32)
-            for piece in halves:
-                nc.tensor.matmul_mx(
-                    out=moments[:, piece], lhsT=z_codes[:, chunk(u)].bitcast(FP8X4), lhsT_scale=z_plane[:, chunk(u)],
-                    rhs=z2_codes[:, piece].bitcast(FP8X4), rhs_scale=z2_plane[:, piece], start=True, stop=True,
-                )
-            for piece in halves:
-                nc.scalar.activation(window[:, piece], moments[:, piece], ACT.Tanh, scale=0.0625)
+        entries = V // LIST_GROUP
+        for i, u in enumerate(order):
             chosen = sbuf("chosen%d" % u, [P, V], F32)
-            nc.vector.tensor_copy(chosen[:], window[:].indirect(cols_list[:]))
+            if i < 3:
+                nc.vector.tensor_copy(chosen[:], window[u][:].indirect(cols_list[:]))
+            else:
+                nc.vector.tensor_copy(chosen[:, 0 : V // 2], window[u][:].indirect(cols_list[:, 0 : entries // 2]))
+                nc.scalar.activation(chosen[:, V // 2 : V], window[u][:].indirect(cols_list[:, entries // 2 : entries]), ACT.Copy)
             nc.sync.dma_start(out=out_rows[:, u, :], in_=chosen[:])

@@ -82,7 +82,7 @@ def tile_picked_selmom_none_p_kernel(tc, x_words, x_scales, wa, wb, gt, gi, offs
             for i, u in enumerate(tiles):
                 nc.scalar.activation(window[u][:, columns], sums[:, i, :], ACT.Tanh, scale=0.0625)
 
-        codes = {name: sbuf(name + "_codes", [P, H], U32) for name in ("wa", "wb", "z", "z2")}
+        codes = {name: sbuf(name + "_codes", [P, H], U32) for name in ("wa", "wb", "z")}
         plane = {name: sbuf(name + "_plane", [P, H], U8) for name in ("wa", "wb", "z", "z2")}
         window = [sbuf("window%d" % u, [P, N], F32) for u in range(PACK)]
         product = {}
@@ -108,37 +108,35 @@ def tile_picked_selmom_none_p_kernel(tc, x_words, x_scales, wa, wb, gt, gi, offs
         nc.sync.dma_start(cols_list[:], cols)
 
         half_bytes = PACK * HALF * 4
-        picked_scales = at("picked_scales", [P, S], U8, half_bytes - 64)
+        picked_room = at("picked_scales", [P, 3 * half_bytes], U8, 0)
+        picked_scales = picked_room[:, 0:S]
         x_plane = sbuf("x_plane", [P, S], U8)
-        nc.vector.tensor_copy(picked_scales[:], scale_table[:].indirect(offs_list[:]))
-        nc.vector.tensor_copy(x_plane[:].rearrange("p (t m) -> p t m", t=PACK), picked_scales[:].rearrange("p (m t) -> p t m", t=PACK))
+        nc.vector.tensor_copy(picked_scales, scale_table[:].indirect(offs_list[:]))
+        nc.vector.tensor_copy(x_plane[:].rearrange("p (t m) -> p t m", t=PACK), picked_scales.rearrange("p (m t) -> p t m", t=PACK))
         for r in range(1, QUADRANT // BLOCK_PARTS):
             nc.sync.dma_start(out=x_plane[:].bitcast(I32)[r:P:QUADRANT, :], in_=x_plane[:].bitcast(I32)[BLOCK_PARTS * r : P : QUADRANT, :])
-        wa_raw = [at("wa_raw0", [P, PACK, HALF], F32, 0), at("wa_raw1", [P, PACK, HALF], F32, half_bytes + 384)]
-        for half in range(2):
-            nc.sync.dma_start(out=wa_raw[half][:], in_=wa_rows[:, :, chunk(2 * half, 2)])
-            if half == 0:
-                gate["wb"] = at("gate_b", [P, PACK], F32, half_bytes + 192)
-                nc.sync.dma_start(out=gate["wb"][:], in_=gi.rearrange("(p t) o -> p (t o)", t=PACK))
-        gate["wa"] = at("gate_a", [P, PACK], F32, half_bytes + 128)
+        wa_raw = [at("wa_raw%d" % half, [P, PACK, HALF], F32, half * half_bytes) for half in range(2)]
+        nc.sync.dma_start(out=wa_raw[0][:], in_=wa_rows[:, :, chunk(0, 2)])
+        gate["wb"] = at("gate_b", [P, PACK], F32, 2 * half_bytes)
+        nc.sync.dma_start(out=gate["wb"][:], in_=gi.rearrange("(p t) o -> p (t o)", t=PACK))
+        nc.sync.dma_start(out=wa_raw[1][:], in_=wa_rows[:, :, chunk(2, 2)])
+        gate["wa"] = at("gate_a", [P, PACK], F32, 2 * half_bytes + 64)
         nc.sync.dma_start(out=gate["wa"][:], in_=gt.rearrange("(p t) o -> p (t o)", t=PACK))
 
-        picked_words = sbuf("picked_words", [P, S], U32)
+        picked_words = at("picked_words", [P, S], U32, 2 * half_bytes + 128)
         x_codes = sbuf("x_codes", [P, S], U32)
         wb_grouped = [sbuf("wb_grouped%d" % c, [P, CHUNK, PACK], BF16) for c in range(PACK)]
         nc.vector.tensor_copy(picked_words[:], word_table[:].indirect(offs_list[:]))
-        round_columns(nc.scalar.copy, wb_grouped[0][:], wb_raw[0][:, :, chunk(0)])
-        round_columns(nc.vector.tensor_copy, wb_grouped[1][:], wb_raw[0][:, :, chunk(1)])
         nc.vector.tensor_copy(
             x_codes[:].rearrange("p (t c i) -> p c t i", t=PACK, i=LINE),
             picked_words[:].rearrange("p (c i t) -> p c t i", t=PACK, i=LINE),
         )
-        for c in range(2):
-            quantize("wb", chunk(c), wb_grouped[c][:])
-            project("wb", c)
-        round_columns(nc.scalar.copy, wb_grouped[2][:], wb_raw[1][:, :, chunk(0)])
+        for c in range(3):
+            round_columns(nc.scalar.copy, wb_grouped[c][:], wb_raw[c // 2][:, :, chunk(c % 2)])
+        quantize("wb", chunk(0), wb_grouped[0][:])
+        project("wb", 0)
         round_columns(nc.vector.tensor_copy, wb_grouped[3][:], wb_raw[1][:, :, chunk(1)])
-        for c in (3, 2):
+        for c in (1, 3, 2):
             quantize("wb", chunk(c), wb_grouped[c][:])
             project("wb", c)
 
@@ -149,46 +147,37 @@ def tile_picked_selmom_none_p_kernel(tc, x_words, x_scales, wa, wb, gt, gi, offs
                 dealt_in = wa_raw[half][:].rearrange("p j (m u) -> p m j u", u=PACK)
                 nc.scalar.copy(dealt_out, dealt_in[:, :, :, 2 * pair : 2 * pair + 2])
 
-        z2_first = sbuf("z2_first", [P, HALF, PACK], BF16)
-        for c in (0, 1):
-            weigh(z2_first[:, chunk(c), :], "wb", c)
-        z2_third = sbuf("z2_third", [P, CHUNK, PACK], BF16)
-        weigh(z2_third[:], "wb", 3)
-        quantize("wa", chunk(0, 2), wa_grouped[0][:].rearrange("p u m j -> p (u m) j"))
-        quantize("z2", chunk(0, 2), z2_first[:])
-        quantize("wa", chunk(2, 2), wa_grouped[1][:].rearrange("p u m j -> p (u m) j"))
-        quantize("z2", chunk(3), z2_third[:])
-        z2_last = sbuf("z2_last", [P, CHUNK, PACK], BF16, after="wa_grouped0")
-        weigh(z2_last[:], "wb", 2)
-        for u in (0, 1, 2, 3):
+        z2_grouped = [sbuf("z2_grouped%d" % half, [P, HALF, PACK], BF16) for half in range(2)]
+        for c in (0, 1, 3, 2):
+            weigh(z2_grouped[c // 2][:, chunk(c % 2), :], "wb", c)
+        for pair in range(2):
+            quantize("wa", chunk(2 * pair, 2), wa_grouped[pair][:].rearrange("p u m j -> p (u m) j"))
+        codes["z2"] = sbuf("z2_codes", [P, N], U32, after="wa_grouped0")
+        quantize("z2", chunk(0, 2), z2_grouped[0][:])
+        for u in range(PACK):
             project("wa", u)
         z_grouped = [sbuf("z_grouped%d" % u, [P, CHUNK, PACK], BF16) for u in range(PACK)]
         rows = {u: weigh_rows("wa", u) for u in (1, 3)}
-        def finish(u):
-            if u in rows:
-                interleave(z_grouped[u][:], rows[u])
-            else:
-                weigh(z_grouped[u][:], "wa", u)
-        order = (0, 1, 2, 3)
-        finish(order[0])
-        quantize("z2", chunk(2), z2_last[:])
-        for i, u in enumerate(order):
-            if 0 < i < 3:
-                finish(order[i + 1])
-            quantize("z", chunk(u), z_grouped[u][:])
-            if i == 0:
-                finish(order[1])
-            if i < 3:
-                moments((u,), chunk(0, 4), "wb_product%d" % i)
-            else:
-                moments((u,), chunk(0, 2), "wb_product%d" % i)
-                moments((u,), chunk(2, 2), "wa_product0")
+        weigh(z_grouped[0][:], "wa", 0)
+        quantize("z2", chunk(2, 2), z2_grouped[1][:])
+        quantize("z", chunk(0), z_grouped[0][:])
+        moments((0,), chunk(0, 4), "wb_product0")
+        interleave(z_grouped[1][:], rows[1])
+        weigh(z_grouped[2][:], "wa", 2)
+        quantize("z", chunk(1), z_grouped[1][:])
+        moments((1,), chunk(0, 4), "wb_product1")
+        interleave(z_grouped[3][:], rows[3])
+        quantize("z", chunk(2), z_grouped[2][:])
+        moments((2,), chunk(0, 4), "wb_product2")
+        quantize("z", chunk(3), z_grouped[3][:])
+        moments((3,), chunk(0, 2), "wb_product3")
+        moments((3,), chunk(2, 2), "wa_product0")
 
         out_rows = out.rearrange("(p u) v -> p u v", u=PACK)
         entries = V // LIST_GROUP
-        for i, u in enumerate(order):
+        for i, u in enumerate((0, 1, 2, 3)):
             chosen = sbuf("chosen%d" % u, [P, V], F32)
-            if i < 3:
+            if i in (0, 1, 2):
                 nc.vector.tensor_copy(chosen[:], window[u][:].indirect(cols_list[:]))
             else:
                 nc.vector.tensor_copy(chosen[:, 0 : V // 2], window[u][:].indirect(cols_list[:, 0 : entries // 2]))

@@ -143,9 +143,9 @@ def tile_picked_selmom_none_p_kernel(tc, x_words, x_scales, wa, wb, gt, gi, offs
         wa_grouped = [sbuf("wa_grouped%d" % pair, [P, 2, CHUNK, PACK], BF16) for pair in range(2)]
         for half in range(2):
             for pair in range(2):
-                dealt_out = wa_grouped[pair][:, :, half * 64 : (half + 1) * 64, :].rearrange("p u m j -> p m j u")
-                dealt_in = wa_raw[half][:].rearrange("p j (m u) -> p m j u", u=PACK)
-                nc.scalar.copy(dealt_out, dealt_in[:, :, :, 2 * pair : 2 * pair + 2])
+                dealt_out = wa_grouped[pair][:, :, half * 64 : (half + 1) * 64, :].rearrange("p u (g i) j -> p u g j i", i=LINE)
+                dealt_in = wa_raw[half][:].rearrange("p j (g u i) -> p u g j i", u=PACK, i=LINE)
+                nc.scalar.copy(dealt_out, dealt_in[:, 2 * pair : 2 * pair + 2])
 
         z2_grouped = [sbuf("z2_grouped%d" % half, [P, HALF, PACK], BF16) for half in range(2)]
         for c in (0, 1, 3, 2):
@@ -162,24 +162,24 @@ def tile_picked_selmom_none_p_kernel(tc, x_words, x_scales, wa, wb, gt, gi, offs
         quantize("z2", chunk(2, 2), z2_grouped[1][:])
         quantize("z", chunk(0), z_grouped[0][:])
         moments((0,), chunk(0, 4), "wb_product0")
-        interleave(z_grouped[1][:], rows[1])
         weigh(z_grouped[2][:], "wa", 2)
-        quantize("z", chunk(1), z_grouped[1][:])
-        moments((1,), chunk(0, 4), "wb_product1")
-        interleave(z_grouped[3][:], rows[3])
+        interleave(z_grouped[1][:], rows[1])
         quantize("z", chunk(2), z_grouped[2][:])
-        moments((2,), chunk(0, 4), "wb_product2")
+        moments((2,), chunk(0, 2), "wb_product1")
+        moments((2,), chunk(2, 2), "wb_product2")
+        interleave(z_grouped[3][:], rows[3])
+        quantize("z", chunk(1), z_grouped[1][:])
+        moments((1,), chunk(0, 4), "wb_product3")
         quantize("z", chunk(3), z_grouped[3][:])
-        moments((3,), chunk(0, 2), "wb_product3")
-        moments((3,), chunk(2, 2), "wa_product0")
+        moments((3,), chunk(0, 4), "wa_product0")
 
-        out_rows = out.rearrange("(p u) v -> p u v", u=PACK)
+        out_rows = out.rearrange("(g u i) v -> u g i v", u=PACK, i=LINE)
         entries = V // LIST_GROUP
-        for i, u in enumerate((0, 1, 2, 3)):
-            chosen = sbuf("chosen%d" % u, [P, V], F32)
+        for i, u in enumerate((0, 2, 1, 3)):
+            chosen = sbuf("chosen%d" % u, [P, V], F32, after="wa_rows3" if i == 0 else None)
             if i in (0, 1, 2):
                 nc.vector.tensor_copy(chosen[:], window[u][:].indirect(cols_list[:]))
             else:
                 nc.vector.tensor_copy(chosen[:, 0 : V // 2], window[u][:].indirect(cols_list[:, 0 : entries // 2]))
                 nc.scalar.activation(chosen[:, V // 2 : V], window[u][:].indirect(cols_list[:, entries // 2 : entries]), ACT.Copy)
-            nc.sync.dma_start(out=out_rows[:, u, :], in_=chosen[:])
+            nc.sync.dma_start(out=out_rows[u], in_=chosen[:])

@@ -150,6 +150,12 @@ def tile_picked_selmom_none_p_kernel(tc, x_words, x_scales, wa, wb, gt, gi, offs
         z2_grouped = [sbuf("z2_grouped%d" % half, [P, HALF, PACK], BF16) for half in range(2)]
         for c in (0, 1, 3, 2):
             weigh(z2_grouped[c // 2][:, chunk(c % 2), :], "wb", c)
+        spare = bank("spare", [P, N], after="wb_product0")
+        for t in range(2):
+            nc.tensor.matmul_mx(
+                out=spare[:], lhsT=x_codes[:, chunk(t)].bitcast(FP8X4), lhsT_scale=x_plane[:, chunk(t)],
+                rhs=codes["wb"][:].bitcast(FP8X4), rhs_scale=plane["wb"][:], start=True, stop=True,
+            )
         for pair in range(2):
             quantize("wa", chunk(2 * pair, 2), wa_grouped[pair][:].rearrange("p u m j -> p (u m) j"))
         codes["z2"] = sbuf("z2_codes", [P, N], U32, after="wa_grouped0")

@@ -175,7 +175,8 @@ def tile_picked_selmom_none_p_kernel(tc, x_words, x_scales, wa, wb, gt, gi, offs
         moments((2,), chunk(2, 2), "wb_product2")
         interleave(z_grouped[3][:], rows[3])
         quantize("z", chunk(1), z_grouped[1][:])
-        moments((1,), chunk(0, 4), "wb_product3")
+        moments((1,), chunk(0, 2), "wb_product3")
+        moments((1,), chunk(2, 2), "wa_product2")
         quantize("z", chunk(3), z_grouped[3][:])
         moments((3,), chunk(0, 4), "wa_product0")
 
@@ -183,9 +184,13 @@ def tile_picked_selmom_none_p_kernel(tc, x_words, x_scales, wa, wb, gt, gi, offs
         entries = V // LIST_GROUP
         for i, u in enumerate((0, 2, 1, 3)):
             chosen = sbuf("chosen%d" % u, [P, V], F32, after="wa_rows3" if i == 0 else None)
-            if i in (0, 1, 2):
+            if i in (0, 1):
                 nc.vector.tensor_copy(chosen[:], window[u][:].indirect(cols_list[:]))
             else:
                 nc.vector.tensor_copy(chosen[:, 0 : V // 2], window[u][:].indirect(cols_list[:, 0 : entries // 2]))
                 nc.scalar.activation(chosen[:, V // 2 : V], window[u][:].indirect(cols_list[:, entries // 2 : entries]), ACT.Copy)
-            nc.sync.dma_start(out=out_rows[u], in_=chosen[:])
+            if i < 3:
+                nc.sync.dma_start(out=out_rows[u], in_=chosen[:])
+            else:
+                nc.sync.dma_start(out=out_rows[u][:, :, 0 : V // 2], in_=chosen[:, 0 : V // 2])
+                nc.scalar.dma_start(out=out_rows[u][:, :, V // 2 : V], in_=chosen[:, V // 2 : V])

@@ -116,9 +116,9 @@ def tile_picked_selmom_none_p_kernel(tc, x_words, x_scales, wa, wb, gt, gi, offs
         for r in range(1, QUADRANT // BLOCK_PARTS):
             nc.sync.dma_start(out=x_plane[:].bitcast(I32)[r:P:QUADRANT, :], in_=x_plane[:].bitcast(I32)[BLOCK_PARTS * r : P : QUADRANT, :])
         wa_raw = [at("wa_raw%d" % half, [P, PACK, HALF], F32, half * half_bytes) for half in range(2)]
-        nc.sync.dma_start(out=wa_raw[0][:], in_=wa_rows[:, :, chunk(0, 2)])
         gate["wb"] = at("gate_b", [P, PACK], F32, 2 * half_bytes)
         nc.sync.dma_start(out=gate["wb"][:], in_=gi.rearrange("(p t) o -> p (t o)", t=PACK))
+        nc.sync.dma_start(out=wa_raw[0][:], in_=wa_rows[:, :, chunk(0, 2)])
         nc.sync.dma_start(out=wa_raw[1][:], in_=wa_rows[:, :, chunk(2, 2)])
         gate["wa"] = at("gate_a", [P, PACK], F32, 2 * half_bytes + 64)
         nc.sync.dma_start(out=gate["wa"][:], in_=gt.rearrange("(p t) o -> p (t o)", t=PACK))

@@ -145,7 +145,11 @@ def tile_picked_selmom_none_p_kernel(tc, x_words, x_scales, wa, wb, gt, gi, offs
             for pair in range(2):
                 dealt_out = wa_grouped[pair][:, :, half * 64 : (half + 1) * 64, :].rearrange("p u (g i) j -> p u g j i", i=LINE)
                 dealt_in = wa_raw[half][:].rearrange("p j (g u i) -> p u g j i", u=PACK, i=LINE)
-                nc.scalar.copy(dealt_out, dealt_in[:, 2 * pair : 2 * pair + 2])
+                if half == 0:
+                    nc.scalar.copy(dealt_out, dealt_in[:, 2 * pair : 2 * pair + 2])
+                else:
+                    for u in range(2):
+                        nc.scalar.copy(dealt_out[:, u], dealt_in[:, 2 * pair + u])
 
         z2_grouped = [sbuf("z2_grouped%d" % half, [P, HALF, PACK], BF16) for half in range(2)]
         for c in (0, 1, 3, 2):
@@ -156,8 +160,8 @@ def tile_picked_selmom_none_p_kernel(tc, x_words, x_scales, wa, wb, gt, gi, offs
                 out=spare[:], lhsT=x_codes[:, chunk(t)].bitcast(FP8X4), lhsT_scale=x_plane[:, chunk(t)],
                 rhs=codes["wb"][:].bitcast(FP8X4), rhs_scale=plane["wb"][:], start=True, stop=True,
             )
-        for pair in range(2):
-            quantize("wa", chunk(2 * pair, 2), wa_grouped[pair][:].rearrange("p u m j -> p (u m) j"))
+        for u in range(PACK):
+            quantize("wa", chunk(u), wa_grouped[u // 2][:, u % 2])
         codes["z2"] = sbuf("z2_codes", [P, N], U32, after="wa_grouped0")
         quantize("z2", chunk(0, 2), z2_grouped[0][:])
         for u in range(PACK):

@@ -169,14 +169,14 @@ def tile_picked_selmom_none_p_kernel(tc, x_words, x_scales, wa, wb, gt, gi, offs
         z_grouped = [sbuf("z_grouped%d" % u, [P, CHUNK, PACK], BF16) for u in range(PACK)]
         rows = {u: weigh_rows("wa", u) for u in (1, 3)}
         weigh(z_grouped[0][:], "wa", 0)
-        quantize("z2", chunk(2, 2), z2_grouped[1][:])
-        quantize("z", chunk(0), z_grouped[0][:])
-        moments((0,), chunk(0, 4), "wb_product0")
         weigh(z_grouped[2][:], "wa", 2)
-        interleave(z_grouped[1][:], rows[1])
+        quantize("z", chunk(0), z_grouped[0][:])
+        moments((0,), chunk(0, 2), "wb_product0")
+        quantize("z2", chunk(2, 2), z2_grouped[1][:])
+        moments((0,), chunk(2, 2), "wb_product1")
         quantize("z", chunk(2), z_grouped[2][:])
-        moments((2,), chunk(0, 2), "wb_product1")
-        moments((2,), chunk(2, 2), "wb_product2")
+        moments((2,), chunk(0, 4), "wb_product2")
+        interleave(z_grouped[1][:], rows[1])
         interleave(z_grouped[3][:], rows[3])
         quantize("z", chunk(1), z_grouped[1][:])
         moments((1,), chunk(0, 2), "wb_product3")

@@ -88,17 +88,21 @@ def tile_picked_selmom_none_p_kernel(tc, x_words, x_scales, wa, wb, gt, gi, offs
         product = {}
         gate = {}
 
+        scale_table = sbuf("scale_table", [P, T], U8)
+        nc.gpsimd.memset(scale_table[:].bitcast(I32)[:, 0:352], 0)
+        nc.vector.memset(scale_table[:].bitcast(I32)[:, 352:512], 0)
         warm = sbuf("warm", [P, 2], F32)
         nc.vector.memset(warm[:, 0:1], 0.0)
         nc.scalar.activation(warm[:, 1:2], warm[:, 0:1], ACT.Tanh)
 
-        scale_table = sbuf("scale_table", [P, T], U8)
         scale_rows = x_scales[0].bitcast(I32)
-        nc.sync.dma_start(out=scale_table[:].bitcast(I32), in_=scale_rows.unsqueeze(1).to_broadcast([P // BLOCK_PARTS, BLOCK_PARTS, T // 4]))
+        word_table = sbuf("word_table", [P, T], U32)
+        word_rows = x_words[0].rearrange("p n t -> p (n t)").bitcast(I32)
+        nc.sync.dma_start(out=word_table[:].bitcast(I32)[:, 0:384], in_=word_rows[:, 0:384])
         offs_list = sbuf("offs_list", [P, S // LIST_GROUP], U16)
         nc.sync.dma_start(offs_list[:], offs)
-        word_table = sbuf("word_table", [P, T], U32)
-        nc.sync.dma_start(out=word_table[:].bitcast(I32), in_=x_words[0].rearrange("p n t -> p (n t)").bitcast(I32))
+        nc.sync.dma_start(out=scale_table[:].bitcast(I32)[0:P:BLOCK_PARTS, :], in_=scale_rows)
+        nc.sync.dma_start(out=word_table[:].bitcast(I32)[:, 384:T], in_=word_rows[:, 384:T])
         wa_rows = wa.rearrange("(p j) h -> p j h", j=PACK)
         wb_rows = wb.rearrange("(p j) n -> p j n", j=PACK)
         wb_raw = [sbuf("wb_raw%d" % half, [P, PACK, HALF], F32) for half in range(2)]
@@ -111,8 +115,14 @@ def tile_picked_selmom_none_p_kernel(tc, x_words, x_scales, wa, wb, gt, gi, offs
         picked_room = at("picked_scales", [P, 3 * half_bytes], U8, 0)
         picked_scales = picked_room[:, 0:S]
         x_plane = sbuf("x_plane", [P, S], U8)
-        nc.vector.tensor_copy(picked_scales, scale_table[:].indirect(offs_list[:]))
-        nc.vector.tensor_copy(x_plane[:].rearrange("p (t m) -> p t m", t=PACK), picked_scales.rearrange("p (m t) -> p t m", t=PACK))
+        halves = [slice(0, HALF), slice(HALF, S)]
+        for half in range(2):
+            nc.vector.tensor_copy(picked_scales[:, halves[half]], scale_table[:].indirect(offs_list[:, 16 * half : 16 * half + 16]))
+        for half in range(2):
+            nc.vector.tensor_copy(
+                x_plane[:].rearrange("p (t m) -> p t m", t=PACK)[:, :, 64 * half : 64 * half + 64],
+                picked_scales[:, halves[half]].rearrange("p (m t) -> p t m", t=PACK),
+            )
         for r in range(1, QUADRANT // BLOCK_PARTS):
             nc.sync.dma_start(out=x_plane[:].bitcast(I32)[r:P:QUADRANT, :], in_=x_plane[:].bitcast(I32)[BLOCK_PARTS * r : P : QUADRANT, :])
         wa_raw = [at("wa_raw%d" % half, [P, PACK, HALF], F32, half * half_bytes) for half in range(2)]
@@ -126,11 +136,13 @@ def tile_picked_selmom_none_p_kernel(tc, x_words, x_scales, wa, wb, gt, gi, offs
         picked_words = at("picked_words", [P, S], U32, 2 * half_bytes + 128)
         x_codes = sbuf("x_codes", [P, S], U32)
         wb_grouped = [sbuf("wb_grouped%d" % c, [P, CHUNK, PACK], BF16) for c in range(PACK)]
-        nc.vector.tensor_copy(picked_words[:], word_table[:].indirect(offs_list[:]))
-        nc.vector.tensor_copy(
-            x_codes[:].rearrange("p (t c i) -> p c t i", t=PACK, i=LINE),
-            picked_words[:].rearrange("p (c i t) -> p c t i", t=PACK, i=LINE),
-        )
+        for half in range(2):
+            nc.vector.tensor_copy(picked_words[:, halves[half]], word_table[:].indirect(offs_list[:, 16 * half : 16 * half + 16]))
+        for half in range(2):
+            nc.vector.tensor_copy(
+                x_codes[:].rearrange("p (t c i) -> p c t i", t=PACK, i=LINE)[:, 16 * half : 16 * half + 16],
+                picked_words[:, halves[half]].rearrange("p (c i t) -> p c t i", t=PACK, i=LINE),
+            )
         for c in range(3):
             round_columns(nc.scalar.copy, wb_grouped[c][:], wb_raw[c // 2][:, :, chunk(c % 2)])
         quantize("wb", chunk(0), wb_grouped[0][:])

@@ -89,8 +89,7 @@ def tile_picked_selmom_none_p_kernel(tc, x_words, x_scales, wa, wb, gt, gi, offs
         gate = {}
 
         scale_table = sbuf("scale_table", [P, T], U8)
-        nc.gpsimd.memset(scale_table[:].bitcast(I32)[:, 0:352], 0)
-        nc.vector.memset(scale_table[:].bitcast(I32)[:, 352:512], 0)
+        nc.vector.memset(scale_table[:].bitcast(I32), 0)
         warm = sbuf("warm", [P, 2], F32)
         nc.vector.memset(warm[:, 0:1], 0.0)
         nc.scalar.activation(warm[:, 1:2], warm[:, 0:1], ACT.Tanh)
@@ -98,11 +97,11 @@ def tile_picked_selmom_none_p_kernel(tc, x_words, x_scales, wa, wb, gt, gi, offs
         scale_rows = x_scales[0].bitcast(I32)
         word_table = sbuf("word_table", [P, T], U32)
         word_rows = x_words[0].rearrange("p n t -> p (n t)").bitcast(I32)
-        nc.sync.dma_start(out=word_table[:].bitcast(I32)[:, 0:384], in_=word_rows[:, 0:384])
+        nc.sync.dma_start(out=word_table[:].bitcast(I32)[:, 0:512], in_=word_rows[:, 0:512])
         offs_list = sbuf("offs_list", [P, S // LIST_GROUP], U16)
         nc.sync.dma_start(offs_list[:], offs)
         nc.sync.dma_start(out=scale_table[:].bitcast(I32)[0:P:BLOCK_PARTS, :], in_=scale_rows)
-        nc.sync.dma_start(out=word_table[:].bitcast(I32)[:, 384:T], in_=word_rows[:, 384:T])
+        nc.sync.dma_start(out=word_table[:].bitcast(I32)[:, 512:T], in_=word_rows[:, 512:T])
         wa_rows = wa.rearrange("(p j) h -> p j h", j=PACK)
         wb_rows = wb.rearrange("(p j) n -> p j n", j=PACK)
         wb_raw = [sbuf("wb_raw%d" % half, [P, PACK, HALF], F32) for half in range(2)]

@@ -114,14 +114,8 @@ def tile_picked_selmom_none_p_kernel(tc, x_words, x_scales, wa, wb, gt, gi, offs
         picked_room = at("picked_scales", [P, 3 * half_bytes], U8, 0)
         picked_scales = picked_room[:, 0:S]
         x_plane = sbuf("x_plane", [P, S], U8)
-        halves = [slice(0, HALF), slice(HALF, S)]
-        for half in range(2):
-            nc.vector.tensor_copy(picked_scales[:, halves[half]], scale_table[:].indirect(offs_list[:, 16 * half : 16 * half + 16]))
-        for half in range(2):
-            nc.vector.tensor_copy(
-                x_plane[:].rearrange("p (t m) -> p t m", t=PACK)[:, :, 64 * half : 64 * half + 64],
-                picked_scales[:, halves[half]].rearrange("p (m t) -> p t m", t=PACK),
-            )
+        nc.vector.tensor_copy(picked_scales, scale_table[:].indirect(offs_list[:]))
+        nc.vector.tensor_copy(x_plane[:].rearrange("p (t m) -> p t m", t=PACK), picked_scales.rearrange("p (m t) -> p t m", t=PACK))
         for r in range(1, QUADRANT // BLOCK_PARTS):
             nc.sync.dma_start(out=x_plane[:].bitcast(I32)[r:P:QUADRANT, :], in_=x_plane[:].bitcast(I32)[BLOCK_PARTS * r : P : QUADRANT, :])
         wa_raw = [at("wa_raw%d" % half, [P, PACK, HALF], F32, half * half_bytes) for half in range(2)]
@@ -135,13 +129,11 @@ def tile_picked_selmom_none_p_kernel(tc, x_words, x_scales, wa, wb, gt, gi, offs
         picked_words = at("picked_words", [P, S], U32, 2 * half_bytes + 128)
         x_codes = sbuf("x_codes", [P, S], U32)
         wb_grouped = [sbuf("wb_grouped%d" % c, [P, CHUNK, PACK], BF16) for c in range(PACK)]
-        for half in range(2):
-            nc.vector.tensor_copy(picked_words[:, halves[half]], word_table[:].indirect(offs_list[:, 16 * half : 16 * half + 16]))
-        for half in range(2):
-            nc.vector.tensor_copy(
-                x_codes[:].rearrange("p (t c i) -> p c t i", t=PACK, i=LINE)[:, 16 * half : 16 * half + 16],
-                picked_words[:, halves[half]].rearrange("p (c i t) -> p c t i", t=PACK, i=LINE),
-            )
+        nc.vector.tensor_copy(picked_words[:], word_table[:].indirect(offs_list[:]))
+        nc.vector.tensor_copy(
+            x_codes[:].rearrange("p (t c i) -> p c t i", t=PACK, i=LINE),
+            picked_words[:].rearrange("p (c i t) -> p c t i", t=PACK, i=LINE),
+        )
         for c in range(3):
             round_columns(nc.scalar.copy, wb_grouped[c][:], wb_raw[c // 2][:, :, chunk(c % 2)])
         quantize("wb", chunk(0), wb_grouped[0][:])

@@ -23,6 +23,7 @@ LINE = 4
 LIST_GROUP = 16
 BLOCK_PARTS = 8
 QUADRANT = 32
+SHARE = 64
 ROWS = CHUNK // PACK
 
 
@@ -68,8 +69,8 @@ def tile_picked_selmom_none_p_kernel(tc, x_words, x_scales, wa, wb, gt, gi, offs
                 nc.scalar.activation(rows[:, t, :], product[name, c][:, t, :], ACT.Copy, scale=gate[name][:, t : t + 1])
             return rows
 
-        def interleave(grouped, rows):
-            nc.vector.tensor_copy(grouped.rearrange("p (g i) t -> p g t i", i=LINE), rows[:].rearrange("p t (g i) -> p g t i", i=LINE))
+        def interleave(copy, grouped, rows):
+            copy(grouped.rearrange("p (g i) t -> p g t i", i=LINE), rows.rearrange("p t (g i) -> p g t i", i=LINE))
 
         def moments(tiles, columns, after):
             width = columns.stop - columns.start
@@ -171,6 +172,7 @@ def tile_picked_selmom_none_p_kernel(tc, x_words, x_scales, wa, wb, gt, gi, offs
             project("wa", u)
         z_grouped = [sbuf("z_grouped%d" % u, [P, CHUNK, PACK], BF16) for u in range(PACK)]
         rows = {u: weigh_rows("wa", u) for u in (1, 3)}
+        interleave(nc.scalar.copy, z_grouped[1][:, 0:SHARE, :], rows[1][:, :, 0:SHARE])
         weigh(z_grouped[0][:], "wa", 0)
         weigh(z_grouped[2][:], "wa", 2)
         quantize("z", chunk(0), z_grouped[0][:])
@@ -179,8 +181,8 @@ def tile_picked_selmom_none_p_kernel(tc, x_words, x_scales, wa, wb, gt, gi, offs
         moments((0,), chunk(2, 2), "wb_product1")
         quantize("z", chunk(2), z_grouped[2][:])
         moments((2,), chunk(0, 4), "wb_product2")
-        interleave(z_grouped[1][:], rows[1])
-        interleave(z_grouped[3][:], rows[3])
+        interleave(nc.vector.tensor_copy, z_grouped[1][:, SHARE:CHUNK, :], rows[1][:, :, SHARE:CHUNK])
+        interleave(nc.vector.tensor_copy, z_grouped[3][:], rows[3][:])
         quantize("z", chunk(1), z_grouped[1][:])
         moments((1,), chunk(0, 2), "wb_product3")
         moments((1,), chunk(2, 2), "wa_product2")

@@ -110,6 +110,8 @@ def tile_picked_selmom_none_p_kernel(tc, x_words, x_scales, wa, wb, gt, gi, offs
             nc.sync.dma_start(out=wb_raw[half][:], in_=wb_rows[:, :, chunk(2 * half, 2)])
         cols_list = sbuf("cols_list", [P, V // LIST_GROUP], U16)
         nc.sync.dma_start(cols_list[:], cols)
+        gate["wb"] = sbuf("gate_b", [P, PACK], F32)
+        nc.sync.dma_start(out=gate["wb"][:], in_=gi.rearrange("(p t) o -> p (t o)", t=PACK))
 
         half_bytes = PACK * HALF * 4
         picked_room = at("picked_scales", [P, 3 * half_bytes], U8, 0)
@@ -118,16 +120,14 @@ def tile_picked_selmom_none_p_kernel(tc, x_words, x_scales, wa, wb, gt, gi, offs
         nc.vector.tensor_copy(picked_scales, scale_table[:].indirect(offs_list[:]))
         nc.vector.tensor_copy(x_plane[:].rearrange("p (t m) -> p t m", t=PACK), picked_scales.rearrange("p (m t) -> p t m", t=PACK))
         for r in range(1, QUADRANT // BLOCK_PARTS):
-            nc.sync.dma_start(out=x_plane[:].bitcast(I32)[r:P:QUADRANT, :], in_=x_plane[:].bitcast(I32)[BLOCK_PARTS * r : P : QUADRANT, :])
+            (nc.scalar if r == 1 else nc.sync).dma_start(out=x_plane[:].bitcast(I32)[r:P:QUADRANT, :], in_=x_plane[:].bitcast(I32)[BLOCK_PARTS * r : P : QUADRANT, :])
         wa_raw = [at("wa_raw%d" % half, [P, PACK, HALF], F32, half * half_bytes) for half in range(2)]
-        gate["wb"] = at("gate_b", [P, PACK], F32, 2 * half_bytes)
-        nc.sync.dma_start(out=gate["wb"][:], in_=gi.rearrange("(p t) o -> p (t o)", t=PACK))
         nc.sync.dma_start(out=wa_raw[0][:], in_=wa_rows[:, :, chunk(0, 2)])
         nc.sync.dma_start(out=wa_raw[1][:], in_=wa_rows[:, :, chunk(2, 2)])
         gate["wa"] = at("gate_a", [P, PACK], F32, 2 * half_bytes + 64)
         nc.sync.dma_start(out=gate["wa"][:], in_=gt.rearrange("(p t) o -> p (t o)", t=PACK))
 
-        picked_words = at("picked_words", [P, S], U32, 2 * half_bytes + 128)
+        picked_words = sbuf("picked_words", [P, S], U32)
         x_codes = sbuf("x_codes", [P, S], U32)
         wb_grouped = [sbuf("wb_grouped%d" % c, [P, CHUNK, PACK], BF16) for c in range(PACK)]
         nc.vector.tensor_copy(picked_words[:], word_table[:].indirect(offs_list[:]))

@@ -24,7 +24,7 @@ LIST_GROUP = 16
 BLOCK_PARTS = 8
 QUADRANT = 32
 SHARE = 64
-ROWS = CHUNK // PACK
+WARM_COLUMNS = 64
 
 
 def tile_picked_selmom_none_p_kernel(tc, x_words, x_scales, wa, wb, gt, gi, offs, cols, out):
@@ -158,10 +158,10 @@ def tile_picked_selmom_none_p_kernel(tc, x_words, x_scales, wa, wb, gt, gi, offs
         z2_grouped = [sbuf("z2_grouped%d" % half, [P, HALF, PACK], BF16) for half in range(2)]
         for c in (0, 1, 3, 2):
             weigh(z2_grouped[c // 2][:, chunk(c % 2), :], "wb", c)
-        spare = bank("spare", [P, N], after="wb_product0")
-        for t in range(2):
+        spare = bank("spare", [WARM_COLUMNS, N], after="wb_product0")
+        for repeat in range(2):
             nc.tensor.matmul_mx(
-                out=spare[:], lhsT=x_codes[:, chunk(t)].bitcast(FP8X4), lhsT_scale=x_plane[:, chunk(t)],
+                out=spare[:], lhsT=codes["wb"][:, 0:WARM_COLUMNS].bitcast(FP8X4), lhsT_scale=plane["wb"][:, 0:WARM_COLUMNS],
                 rhs=codes["wb"][:].bitcast(FP8X4), rhs_scale=plane["wb"][:], start=True, stop=True,
             )
         for u in range(PACK):

@@ -198,8 +198,4 @@ def tile_picked_selmom_none_p_kernel(tc, x_words, x_scales, wa, wb, gt, gi, offs
             else:
                 nc.vector.tensor_copy(chosen[:, 0 : V // 2], window[u][:].indirect(cols_list[:, 0 : entries // 2]))
                 nc.scalar.activation(chosen[:, V // 2 : V], window[u][:].indirect(cols_list[:, entries // 2 : entries]), ACT.Copy)
-            if i < 3:
-                nc.sync.dma_start(out=out_rows[u], in_=chosen[:])
-            else:
-                nc.sync.dma_start(out=out_rows[u][:, :, 0 : V // 2], in_=chosen[:, 0 : V // 2])
-                nc.scalar.dma_start(out=out_rows[u][:, :, V // 2 : V], in_=chosen[:, V // 2 : V])
+            nc.sync.dma_start(out=out_rows[u], in_=chosen[:])

@@ -24,7 +24,6 @@ LIST_GROUP = 16
 BLOCK_PARTS = 8
 QUADRANT = 32
 SHARE = 64
-WARM_COLUMNS = 64
 
 
 def tile_picked_selmom_none_p_kernel(tc, x_words, x_scales, wa, wb, gt, gi, offs, cols, out):
@@ -158,12 +157,6 @@ def tile_picked_selmom_none_p_kernel(tc, x_words, x_scales, wa, wb, gt, gi, offs
         z2_grouped = [sbuf("z2_grouped%d" % half, [P, HALF, PACK], BF16) for half in range(2)]
         for c in (0, 1, 3, 2):
             weigh(z2_grouped[c // 2][:, chunk(c % 2), :], "wb", c)
-        spare = bank("spare", [WARM_COLUMNS, N], after="wb_product0")
-        for repeat in range(2):
-            nc.tensor.matmul_mx(
-                out=spare[:], lhsT=codes["wb"][:, 0:WARM_COLUMNS].bitcast(FP8X4), lhsT_scale=plane["wb"][:, 0:WARM_COLUMNS],
-                rhs=codes["wb"][:].bitcast(FP8X4), rhs_scale=plane["wb"][:], start=True, stop=True,
-            )
         for u in range(PACK):
             quantize("wa", chunk(u), wa_grouped[u // 2][:, u % 2])
         codes["z2"] = sbuf("z2_codes", [P, N], U32, after="wa_grouped0")

from contextlib import ExitStack

import concourse.mybir as mybir

K, T, S, V, N, H = 512, 2048, 512, 256, 512, 512
FLOPS = 2 * K * S * H + 2 * K * S * N + 2 * S * H * N

F32 = mybir.dt.float32
BF16 = mybir.dt.bfloat16
I32 = mybir.dt.int32
U32 = mybir.dt.uint32
U16 = mybir.dt.uint16
U8 = mybir.dt.uint8
FP8X4 = mybir.dt.float8_e4m3fn_x4
ACT = mybir.ActivationFunctionType
MULT = mybir.AluOpType.mult

P = 128
PACK = 4
CHUNK = 128
HALF = 2 * CHUNK
LINE = 4
LIST_GROUP = 16
BLOCK_PARTS = 8
QUADRANT = 32
SHARE = 64


def tile_picked_selmom_none_p_kernel(tc, x_words, x_scales, wa, wb, gt, gi, offs, cols, out):
    nc = tc.nc
    with ExitStack() as ctx:
        held = ctx.enter_context(tc.tile_pool(name="held", bufs=1))
        placed = ctx.enter_context(tc.tile_pool(name="placed", bufs=1))
        psum = ctx.enter_context(tc.psum_pool(name="psum", bufs=1))

        def sbuf(name, shape, dtype, after=None):
            return held.tile(shape, dtype, name=name, tag=after or name, align_bytes=64)

        def at(name, shape, dtype, offset):
            return placed.tile(shape, dtype, name=name, tag=name, align_bytes=64, offset=offset)

        def bank(name, shape, after=None):
            return psum.tile(shape, F32, name=name, tag=after or name)

        def chunk(c, count=1):
            return slice(c * CHUNK, (c + count) * CHUNK)

        def quantize(name, columns, grouped):
            nc.vector.quantize_mx(out=codes[name][:, columns].bitcast(FP8X4), scales=plane[name][:, columns], in_=grouped.rearrange("p n t -> p (n t)"))

        def round_columns(copy, grouped, raw):
            copy(grouped.rearrange("p (g i) j -> p g j i", i=LINE), raw.rearrange("p j (g i) -> p g j i", i=LINE))

        def project(name, c, after=None):
            product[name, c] = bank("%s_product%d" % (name, c), [P, PACK, CHUNK], after=after)
            for t in range(PACK):
                nc.tensor.matmul_mx(
                    out=product[name, c][:, t, :], lhsT=x_codes[:, chunk(t)].bitcast(FP8X4), lhsT_scale=x_plane[:, chunk(t)],
                    rhs=codes[name][:, chunk(c)].bitcast(FP8X4), rhs_scale=plane[name][:, chunk(c)], start=True, stop=True,
                )

        def weigh(grouped, name, c):
            nc.vector.tensor_tensor(grouped, product[name, c][:].rearrange("p t n -> p n t"), gate[name][:].unsqueeze(1).to_broadcast([P, CHUNK, PACK]), MULT)

        def weigh_rows(name, c, after=None):
            rows = sbuf("%s_rows%d" % (name, c), [P, PACK, CHUNK], BF16, after=after)
            for t in range(PACK):
                nc.scalar.activation(rows[:, t, :], product[name, c][:, t, :], ACT.Copy, scale=gate[name][:, t : t + 1])
            return rows

        def interleave(copy, grouped, rows):
            copy(grouped.rearrange("p (g i) t -> p g t i", i=LINE), rows.rearrange("p t (g i) -> p g t i", i=LINE))

        def moments(tiles, columns, after):
            width = columns.stop - columns.start
            sums = bank("moments%d_%d" % (tiles[0], columns.start), [P, len(tiles), width], after=after)
            for i, u in enumerate(tiles):
                nc.tensor.matmul_mx(
                    out=sums[:, i, :], lhsT=codes["z"][:, chunk(u)].bitcast(FP8X4), lhsT_scale=plane["z"][:, chunk(u)],
                    rhs=codes["z2"][:, columns].bitcast(FP8X4), rhs_scale=plane["z2"][:, columns], start=True, stop=True,
                )
            for i, u in enumerate(tiles):
                nc.scalar.activation(window[u][:, columns], sums[:, i, :], ACT.Tanh, scale=0.0625)

        codes = {name: sbuf(name + "_codes", [P, H], U32) for name in ("wa", "wb", "z")}
        plane = {name: sbuf(name + "_plane", [P, H], U8) for name in ("wa", "wb", "z", "z2")}
        window = [sbuf("window%d" % u, [P, N], F32) for u in range(PACK)]
        product = {}
        gate = {}

        scale_table = sbuf("scale_table", [P, T], U8)
        nc.vector.memset(scale_table[:].bitcast(I32), 0)
        warm = sbuf("warm", [P, 2], F32)
        nc.vector.memset(warm[:, 0:1], 0.0)
        nc.scalar.activation(warm[:, 1:2], warm[:, 0:1], ACT.Tanh)

        scale_rows = x_scales[0].bitcast(I32)
        word_table = sbuf("word_table", [P, T], U32)
        word_rows = x_words[0].rearrange("p n t -> p (n t)").bitcast(I32)
        nc.sync.dma_start(out=word_table[:].bitcast(I32)[:, 0:512], in_=word_rows[:, 0:512])
        offs_list = sbuf("offs_list", [P, S // LIST_GROUP], U16)
        nc.sync.dma_start(offs_list[:], offs)
        nc.sync.dma_start(out=scale_table[:].bitcast(I32)[0:P:BLOCK_PARTS, :], in_=scale_rows)
        nc.sync.dma_start(out=word_table[:].bitcast(I32)[:, 512:T], in_=word_rows[:, 512:T])
        wa_rows = wa.rearrange("(p j) h -> p j h", j=PACK)
        wb_rows = wb.rearrange("(p j) n -> p j n", j=PACK)
        wb_raw = [sbuf("wb_raw%d" % half, [P, PACK, HALF], F32) for half in range(2)]
        for half in range(2):
            nc.sync.dma_start(out=wb_raw[half][:], in_=wb_rows[:, :, chunk(2 * half, 2)])
        cols_list = sbuf("cols_list", [P, V // LIST_GROUP], U16)
        nc.sync.dma_start(cols_list[:], cols)
        gate["wb"] = sbuf("gate_b", [P, PACK], F32)
        nc.sync.dma_start(out=gate["wb"][:], in_=gi.rearrange("(p t) o -> p (t o)", t=PACK))

        half_bytes = PACK * HALF * 4
        picked_room = at("picked_scales", [P, 3 * half_bytes], U8, 0)
        picked_scales = picked_room[:, 0:S]
        x_plane = sbuf("x_plane", [P, S], U8)
        nc.vector.tensor_copy(picked_scales, scale_table[:].indirect(offs_list[:]))
        nc.vector.tensor_copy(x_plane[:].rearrange("p (t m) -> p t m", t=PACK), picked_scales.rearrange("p (m t) -> p t m", t=PACK))
        for r in range(1, QUADRANT // BLOCK_PARTS):
            (nc.scalar if r == 1 else nc.sync).dma_start(out=x_plane[:].bitcast(I32)[r:P:QUADRANT, :], in_=x_plane[:].bitcast(I32)[BLOCK_PARTS * r : P : QUADRANT, :])
        wa_raw = [at("wa_raw%d" % half, [P, PACK, HALF], F32, half * half_bytes) for half in range(2)]
        nc.sync.dma_start(out=wa_raw[0][:], in_=wa_rows[:, :, chunk(0, 2)])
        nc.sync.dma_start(out=wa_raw[1][:], in_=wa_rows[:, :, chunk(2, 2)])
        gate["wa"] = at("gate_a", [P, PACK], F32, 2 * half_bytes + 64)
        nc.sync.dma_start(out=gate["wa"][:], in_=gt.rearrange("(p t) o -> p (t o)", t=PACK))

        picked_words = sbuf("picked_words", [P, S], U32)
        x_codes = sbuf("x_codes", [P, S], U32)
        wb_grouped = [sbuf("wb_grouped%d" % c, [P, CHUNK, PACK], BF16) for c in range(PACK)]
        nc.vector.tensor_copy(picked_words[:], word_table[:].indirect(offs_list[:]))
        nc.vector.tensor_copy(
            x_codes[:].rearrange("p (t c i) -> p c t i", t=PACK, i=LINE),
            picked_words[:].rearrange("p (c i t) -> p c t i", t=PACK, i=LINE),
        )
        for c in range(3):
            round_columns(nc.scalar.copy, wb_grouped[c][:], wb_raw[c // 2][:, :, chunk(c % 2)])
        quantize("wb", chunk(0), wb_grouped[0][:])
        project("wb", 0)
        round_columns(nc.vector.tensor_copy, wb_grouped[3][:], wb_raw[1][:, :, chunk(1)])
        for c in (1, 3, 2):
            quantize("wb", chunk(c), wb_grouped[c][:])
            project("wb", c)

        wa_grouped = [sbuf("wa_grouped%d" % pair, [P, 2, CHUNK, PACK], BF16) for pair in range(2)]
        for half in range(2):
            for pair in range(2):
                dealt_out = wa_grouped[pair][:, :, half * 64 : (half + 1) * 64, :].rearrange("p u (g i) j -> p u g j i", i=LINE)
                dealt_in = wa_raw[half][:].rearrange("p j (g u i) -> p u g j i", u=PACK, i=LINE)
                if half == 0:
                    nc.scalar.copy(dealt_out, dealt_in[:, 2 * pair : 2 * pair + 2])
                else:
                    for u in range(2):
                        nc.scalar.copy(dealt_out[:, u], dealt_in[:, 2 * pair + u])

        z2_grouped = [sbuf("z2_grouped%d" % half, [P, HALF, PACK], BF16) for half in range(2)]
        for c in (0, 1, 3, 2):
            weigh(z2_grouped[c // 2][:, chunk(c % 2), :], "wb", c)
        for u in range(PACK):
            quantize("wa", chunk(u), wa_grouped[u // 2][:, u % 2])
        codes["z2"] = sbuf("z2_codes", [P, N], U32, after="wa_grouped0")
        quantize("z2", chunk(0, 2), z2_grouped[0][:])
        for u in range(PACK):
            project("wa", u)
        z_grouped = [sbuf("z_grouped%d" % u, [P, CHUNK, PACK], BF16) for u in range(PACK)]
        rows = {u: weigh_rows("wa", u) for u in (1, 3)}
        interleave(nc.scalar.copy, z_grouped[1][:, 0:SHARE, :], rows[1][:, :, 0:SHARE])
        weigh(z_grouped[0][:], "wa", 0)
        weigh(z_grouped[2][:], "wa", 2)
        quantize("z", chunk(0), z_grouped[0][:])
        moments((0,), chunk(0, 2), "wb_product0")
        quantize("z2", chunk(2, 2), z2_grouped[1][:])
        moments((0,), chunk(2, 2), "wb_product1")
        quantize("z", chunk(2), z_grouped[2][:])
        moments((2,), chunk(0, 4), "wb_product2")
        interleave(nc.vector.tensor_copy, z_grouped[1][:, SHARE:CHUNK, :], rows[1][:, :, SHARE:CHUNK])
        interleave(nc.vector.tensor_copy, z_grouped[3][:], rows[3][:])
        quantize("z", chunk(1), z_grouped[1][:])
        moments((1,), chunk(0, 2), "wb_product3")
        moments((1,), chunk(2, 2), "wa_product2")
        quantize("z", chunk(3), z_grouped[3][:])
        moments((3,), chunk(0, 4), "wa_product0")

        out_rows = out.rearrange("(g u i) v -> u g i v", u=PACK, i=LINE)
        entries = V // LIST_GROUP
        for i, u in enumerate((0, 2, 1, 3)):
            chosen = sbuf("chosen%d" % u, [P, V], F32, after="wa_rows3" if i == 0 else None)
            if i in (0, 1):
                nc.vector.tensor_copy(chosen[:], window[u][:].indirect(cols_list[:]))
            else:
                nc.vector.tensor_copy(chosen[:, 0 : V // 2], window[u][:].indirect(cols_list[:, 0 : entries // 2]))
                nc.scalar.activation(chosen[:, V // 2 : V], window[u][:].indirect(cols_list[:, entries // 2 : entries]), ACT.Copy)
            nc.sync.dma_start(out=out_rows[u], in_=chosen[:])
